import numpy as np
import ml_dtypes


def mxq(x, axis, fmt="e4m3"):
    dtype, down = {"e4m3": (ml_dtypes.float8_e4m3fn, 7), "e5m2": (ml_dtypes.float8_e5m2, 14)}[fmt]
    v = np.moveaxis(np.asarray(x, np.float32).astype(ml_dtypes.bfloat16).astype(np.float64), axis, -1)
    blocks = v.reshape(v.shape[:-1] + (-1, 32))
    amax = np.abs(blocks).max(-1, keepdims=True)
    byte = np.maximum(np.where(amax > 0, np.frexp(amax)[1] - 1 + 127, 0) - down, 1)
    scale = np.exp2(byte - 127.0)
    codes = (blocks / scale).astype(np.float32).astype(dtype).astype(np.float64)
    return np.moveaxis((codes * scale).reshape(v.shape), -1, axis)


WIDE = False


def mx_kscale(k):
    if not WIDE:
        return np.ones(k)
    levels = np.array([10, -10, 5, -5, 0])
    if k % 512:
        return np.exp2(np.random.permutation(np.resize(levels, k // 32))).repeat(32)
    a = np.empty((k // 512, 16))
    for p in range(k // 512):
        a[p, :8] = np.random.permutation(np.resize(levels, 8))
        for g in range(8):
            far = levels[np.abs(levels - a[p, g]) >= 10]
            a[p, g + 8] = far[np.random.randint(len(far))]
    return np.exp2(a.ravel()).repeat(32)


def f64(x):
    return np.asarray(x).astype(np.float64)


def striped(idx):
    return np.tile(idx.reshape(-1, 16).T, (8, 1)).astype(np.uint16)


def unstriped(offs):
    return offs[:16].T.reshape(-1).astype(np.int64)


E2M1 = np.array([0.0, 0.5, 1.0, 1.5, 2.0, 3.0, 4.0, 6.0, -0.0, -0.5, -1.0, -1.5, -2.0, -3.0, -4.0, -6.0])


def pack_weight(w, fmt):
    k, n = w.shape
    w = f64(np.asarray(w, np.float32).astype(ml_dtypes.bfloat16)).reshape(k // 32, 32, n)
    amax = np.abs(w).max(1)
    if fmt == "e4m3":
        byte = np.frexp(amax)[1] - 1 + 127 - 7
    else:
        mant, ex = np.frexp(amax / 6.0)
        byte = np.where(mant > 0.5, ex, ex - 1) + 127
    byte = np.clip(np.where(amax > 0, byte, 1), 1, 254)
    scaled = (w * np.exp2(127.0 - byte)[:, None, :]).reshape(k, n).astype(np.float32)
    by_word = np.ascontiguousarray(scaled.reshape(k // 512, 128, 4, n).transpose(0, 1, 3, 2))
    if fmt == "e4m3":
        words = by_word.astype(ml_dtypes.float8_e4m3fn).view(np.uint8)
    else:
        c = by_word.astype(ml_dtypes.float4_e2m1fn).view(np.uint8) & 0xF
        words = (c[..., 0::2] | (c[..., 1::2] << 4)).reshape(k // 512, 128, 2 * n)
    return np.ascontiguousarray(words), np.ascontiguousarray(byte.astype(np.uint8).reshape(k // 512, 16, n))


def unpack_weight(words, scales, fmt):
    g, _, n = scales.shape
    words = np.ascontiguousarray(words).reshape(g, 128, n, -1)
    if fmt == "e4m3":
        vals = words.view(ml_dtypes.float8_e4m3fn).astype(np.float64)
    else:
        nib = np.empty((g, 128, n, 4), np.uint8)
        nib[..., 0::2] = words & 0xF
        nib[..., 1::2] = words >> 4
        vals = E2M1[nib]
    vals = vals * np.repeat(np.exp2(scales.astype(np.float64) - 127.0), 8, axis=1)[..., None]
    return vals.transpose(0, 1, 3, 2).reshape(g * 512, n)


def planes(y):
    n, m = y.shape
    v = y.astype(np.float32).astype(ml_dtypes.bfloat16).astype(np.float64).reshape(n // 32, 32, m)
    top = np.abs(v).max(1)
    byte = np.clip(np.where(top > 0, np.frexp(top)[1] - 1 + 127 - 7, 1), 1, 254)
    codes = (v * np.exp2(127.0 - byte)[:, None, :]).reshape(n, m).astype(np.float32).astype(ml_dtypes.float8_e4m3fn).view(np.uint8)
    words = codes.reshape(n // 512, 128, 4, m).transpose(0, 1, 3, 2)
    return np.ascontiguousarray(words), np.ascontiguousarray(byte.astype(np.uint8).reshape(n // 512, 16, m))


K, T, E, C, H, N = 512, 512, 8, 128, 512, 1024


def by_expert(wq, xq):
    return np.concatenate([wq[e].T @ xq[:, e * C:(e + 1) * C] for e in range(E)], axis=1)


def setup_inputs():
    n = np.random.standard_normal
    v = mx_kscale(N)
    u = mx_kscale(H)
    first = np.random.permutation(np.repeat(np.arange(E), T // E))
    second = (first + 1 + np.random.permutation(np.repeat(np.arange(E - 1), -(-T // (E - 1)))[:T])) % E
    while np.bincount(second, minlength=E).max() != T // E:
        load = np.bincount(second, minlength=E); hi, lo = int(load.argmax()), int(load.argmin())
        t = np.flatnonzero((second == hi) & (first != lo))[0]; second[t] = lo
    slot_token = np.empty(E * C, np.int64); pos = np.empty((2, T), np.int64); fill = np.zeros(E, np.int64)
    place = np.stack([np.random.permutation(C) for _ in range(E)])
    for r, deal in enumerate((first, second)):
        for t in np.random.permutation(T):
            e = deal[t]; j = e * C + place[e, fill[e]]; fill[e] += 1; slot_token[j] = t; pos[r, t] = j
    g = np.random.uniform(0.2, 0.8, T)
    w_slot = np.empty(E * C); w_slot[pos[0]] = g; w_slot[pos[1]] = 1.0 - g
    dy = pack_weight(n((N, T)) * v[:, None], "e4m3")
    wbt = [pack_weight(m, "e2m1") for m in n((E, N, H)) / np.sqrt(N) / v[None, :, None] * u]
    wat = [pack_weight(m, "e2m1") for m in n((E, H, K)) / np.sqrt(H) / u[None, :, None]]
    return {
        "dy_words": dy[0],
        "dy_scales": dy[1],
        "wt": (n((N, K)) / np.sqrt(N) / v[:, None]).astype(np.float32),
        "wbt_words": np.stack([m[0] for m in wbt]),
        "wbt_scales": np.stack([m[1] for m in wbt]),
        "wat_words": np.stack([m[0] for m in wat]),
        "wat_scales": np.stack([m[1] for m in wat]),
        "gate": (np.tile(w_slot, (128, 1))).astype(np.float32),
        "offs": striped(slot_token),
        "pos1": striped(pos[0]),
        "pos2": striped(pos[1]),
    }


def reference(dy_words, dy_scales, wt, wbt_words, wbt_scales, wat_words, wat_scales, gate, offs, pos1, pos2):
    wtq = mxq(f64(wt), 0, "e4m3")
    wbt = np.stack([unpack_weight(wbt_words[e], wbt_scales[e], "e2m1") for e in range(E)])
    wat = np.stack([unpack_weight(wat_words[e], wat_scales[e], "e2m1") for e in range(E)])
    idx = unstriped(offs)
    dy = unpack_weight(dy_words, dy_scales, "e4m3")
    base = wtq.T @ dy
    dh = f64(gate[:1]) * by_expert(wbt, dy[:, idx])
    dx = by_expert(wat, mxq(dh, 0, "e4m3"))
    c = dx[:, unstriped(pos1)] + dx[:, unstriped(pos2)]
    out_0 = base + c
    return (out_0,) + planes(out_0)

@@ -1,0 +1,258 @@
+from contextlib import ExitStack
+
+import concourse.mybir as mybir
+
+K, T, E, C, H, N = 512, 512, 8, 128, 512, 1024
+S = E * C
+P = 128
+PASSES = 2
+PAIRS = E // 2
+FLOPS = 2 * N * K * T + 2 * N * H * S + 2 * H * K * S
+
+F32 = mybir.dt.float32
+BF16 = mybir.dt.bfloat16
+I32 = mybir.dt.int32
+U32 = mybir.dt.uint32
+U16 = mybir.dt.uint16
+U8 = mybir.dt.uint8
+FP8X4 = mybir.dt.float8_e4m3fn_x4
+FP4X4 = mybir.dt.float4_e2m1fn_x4
+COPY = mybir.ActivationFunctionType.Copy
+ADD = mybir.AluOpType.add
+
+
+def tile_moe_adb_none_kernel(
+    tc, dy_words, dy_scales, wt, wbt_words, wbt_scales, wat_words, wat_scales, gate, offs, pos1, pos2,
+    out_0, out_1, out_2,
+):
+    nc = tc.nc
+    with ExitStack() as ctx:
+        keep = ctx.enter_context(tc.tile_pool(name="keep", bufs=1))
+        laid = ctx.enter_context(tc.tile_pool(name="laid", bufs=1))
+        psum = ctx.enter_context(tc.psum_pool(name="psum", bufs=1))
+
+        def sb(shape, dtype, name):
+            return keep.tile(shape, dtype, name=name, align_bytes=64)
+
+        def bank(tag, bufs, name):
+            return psum.tile([P, 512], F32, name=name, tag=tag, bufs=bufs)
+
+        offs_sb = keep.tile([P, S // 16], U16, name="offs_sb")
+        pos1_sb = keep.tile([P, T // 16], U16, name="pos1_sb")
+        pos2_sb = keep.tile([P, T // 16], U16, name="pos2_sb")
+        dyw_all = sb([P, PASSES * T], I32, "dyw_all")
+        dyw = [dyw_all[:, T * s:T * (s + 1)] for s in range(PASSES)]
+        dys = sb([P, PASSES, T], U8, "dys")
+        wbs0 = sb([P, 2 * PASSES, H], U8, "wbs0")
+        wbs1 = sb([P, (E - 2) * PASSES, H], U8, "wbs1")
+        was = sb([P, E, K], U8, "was")
+        blank = laid.tile([P, P], F32, name="blank", align_bytes=64, offset=65536 - 256)
+        wbw0 = sb([P, 4096], U8, "wbw0")
+        ident = sb([P, P], F32, "ident")
+        grow_area = laid.tile([P, 8192 + 1280], F32, name="grow_area", align_bytes=64, offset=16384)
+        grow = grow_area[:, 0:P]
+        gcol = sb([P, E], F32, "gcol")
+
+        nc.gpsimd.memset(dys[:].bitcast(I32), 0)
+        nc.gpsimd.memset(grow, 0.0)
+        nc.gpsimd.memset(blank[:], 0.0)
+        nc.gpsimd.affine_select(out=ident[:], in_=blank[:], compare_op=mybir.AluOpType.not_equal, fill=1.0,
+                                base=0, pattern=[[-1, P]], channel_multiplier=1)
+        nc.vector.memset(wbs0[:].bitcast(I32), 0)
+        nc.vector.memset(wbs1[:].bitcast(I32), 0)
+        nc.vector.memset(was[:].bitcast(I32), 0)
+
+        def load_scales(eng, plane, rows):
+            for r in range(4):
+                eng.dma_start(out=plane[r:P:32].bitcast(I32), in_=rows[r].bitcast(I32))
+
+        nc.sync.dma_start(offs_sb[:], offs)
+        nc.sync.dma_start(out=dyw_all[:].rearrange("p (s t) -> p s t", s=PASSES),
+                          in_=dy_words.rearrange("s p t d -> p s (t d)").bitcast(I32))
+        nc.sync.dma_start(pos1_sb[:], pos1)
+        nc.sync.dma_start(pos2_sb[:], pos2)
+        nc.sync.dma_start(out=wbw0[:].bitcast(I32).rearrange("p (x c) -> p x c", x=4),
+                          in_=wbt_words[0:2].rearrange("e s p c -> p (e s) c").bitcast(I32))
+        load_scales(nc.sync, dys, dy_scales.rearrange("s (q r) t -> r q s t", r=4))
+        nc.sync.dma_start(out=grow_area[0:E, 0:P], in_=gate[0:1, :].rearrange("o (e u) -> (o e) u", u=C))
+        load_scales(nc.sync, wbs0, wbt_scales[0:2].rearrange("e s (q r) c -> r q (e s) c", r=4))
+        gbank = bank("w", 2, "gbank")
+        nc.tensor.transpose(gbank[:, 0:P], grow, ident[:])
+        nc.scalar.activation(out=gcol[:], in_=gbank[:, 0:E], func=COPY)
+
+        wraw = [laid.tile([P, 1024], F32, name="wraw%d" % q, align_bytes=64, offset=32768 + 4096 * q)
+                for q in range(4)]
+        wbw1 = laid.tile([P, 4096], U8, name="wbw1", align_bytes=64, offset=65536)
+        wb_words = [wbw0[:], wbw1[:]] + [
+            laid.tile([P, 4096], U8, name="wbw%d" % j, align_bytes=64, offset=16384 + 4096 * (j - 2))[:]
+            for j in (2, 3)]
+        wa_words = [laid.tile([P, 2048], U8, name="waw%d" % j, align_bytes=64, offset=24576 + 2048 * j)[:]
+                    for j in range(PAIRS)]
+
+        def load_wb(j):
+            nc.sync.dma_start(out=wb_words[j].bitcast(I32).rearrange("p (x c) -> p x c", x=4),
+                              in_=wbt_words[2 * j:2 * j + 2].rearrange("e s p c -> p (e s) c").bitcast(I32))
+
+        def load_wa(j):
+            nc.sync.dma_start(out=wa_words[j].bitcast(I32).rearrange("p (x c) -> p x c", x=2),
+                              in_=wat_words[2 * j:2 * j + 2].rearrange("e s p c -> p (e s) c").bitcast(I32))
+
+        def load_wt(q):
+            s, half = divmod(q, 2)
+            rows = wt[512 * s:512 * (s + 1), 256 * half:256 * (half + 1)]
+            nc.sync.dma_start(out=wraw[q][:].rearrange("p (j c) -> p j c", j=4),
+                              in_=rows.rearrange("(p j) c -> p j c", j=4))
+
+        load_wb(1)
+        load_scales(nc.sync, wbs1, wbt_scales[2:E].rearrange("e s (q r) c -> r q (e s) c", r=4))
+        load_scales(nc.sync, was, wat_scales.rearrange("e s (q r) c -> r q (e s) c", r=4))
+        load_wa(0)
+        load_wb(2)
+        load_wa(1)
+        load_wt(0)
+        load_wb(3)
+        load_wt(1)
+        load_wa(2)
+        load_wt(2)
+        load_wt(3)
+        load_wa(3)
+
+        gw = {}
+        gs = {}
+
+        def gather(j, s, word_at=None, byte_at=None):
+            if word_at is None:
+                gw[j, s] = sb([P, 2 * C], U32, "gw%d%d" % (j, s))
+                gs[j, s] = sb([P, 2 * C], U8, "gs%d%d" % (j, s))
+            else:
+                gw[j, s] = laid.tile([P, 2 * C], U32, name="gw%d%d" % (j, s), align_bytes=64, offset=word_at)
+                gs[j, s] = laid.tile([P, 2 * C], U8, name="gs%d%d" % (j, s), align_bytes=64, offset=byte_at)
+            cut = offs_sb[:, 16 * j:16 * (j + 1)]
+            nc.vector.tensor_copy(out=gw[j, s][:], in_=dyw[s].bitcast(U32).indirect(cut))
+            nc.vector.tensor_copy(out=gs[j, s][:], in_=dys[:, s, :].indirect(cut))
+
+        dx = [sb([P, S], F32, "dx%d" % b) for b in range(4)]
+
+        gather(0, 0)
+        gather(0, 1)
+        for j in (1, 2):
+            for s in range(PASSES):
+                at = 49152 + 1280 * (2 * (j - 1) + s)
+                gather(j, s, at, at + 1024)
+        for j in range(PAIRS):
+            wbank = bank("w", 2, "wbank%d" % j)
+            for ee in range(2):
+                e = 2 * j + ee
+                hbank = bank("h", 3, "hbank%d" % e)
+                slots = slice(C * ee, C * (ee + 1))
+                for s in range(PASSES):
+                    nc.tensor.matmul_mx(
+                        out=hbank[:], lhsT=gw[j, s][:, slots].bitcast(FP8X4), lhsT_scale=gs[j, s][:, slots],
+                        rhs=wb_words[j][:, 1024 * (2 * ee + s):1024 * (2 * ee + s + 1)].bitcast(FP4X4),
+                        rhs_scale=(wbs0[:, 2 * e + s, :] if j == 0 else wbs1[:, 2 * e + s - 4, :]),
+                        start=(s == 0), stop=(s == PASSES - 1))
+                dht = sb([P, H], BF16, "dht%d" % e)
+                nc.scalar.activation(
+                    out=dht[:].rearrange("c (u p h) -> c u p h", u=2, h=2),
+                    in_=hbank[:].rearrange("c (p u h) -> c u p h", u=2, h=2),
+                    func=COPY, scale=gcol[:, e:e + 1])
+                words = dht[:].bitcast(F32)
+                for u in range(2):
+                    at = P * (2 * ee + u)
+                    nc.tensor.transpose(wbank[:, at:at + P], words[:, P * u:P * (u + 1)], ident[:])
+            dhb = laid.tile([P, 4 * 2 * C], BF16, name="dhb%d" % j, align_bytes=64, offset=4096 * j + 512)
+            nc.scalar.copy(
+                out=dhb[:].bitcast(F32).rearrange("p (x c u) -> p x c u", x=2, u=2),
+                in_=wbank[:].rearrange("p (x u c) -> p x c u", x=2, u=2))
+            hc = sb([P, 2 * C], U32, "hc%d" % j)
+            hs = sb([P, 2 * C], U8, "hs%d" % j)
+            nc.vector.quantize_mx(out=hc[:].bitcast(FP8X4), scales=hs[:], in_=dhb[:])
+            if j == 0:
+                gather(3, 0, 0, 1024)
+                gather(3, 1, 1536, 1280)
+            for bb in range(2):
+                dbank = bank("d", 3, "dbank%d%d" % (j, bb))
+                for b in (2 * bb, 2 * bb + 1):
+                    for ee in range(2):
+                        e = 2 * j + ee
+                        at = 2 * C * (b % 2) + C * ee
+                        slots = slice(C * ee, C * (ee + 1))
+                        nc.tensor.matmul_mx(
+                            out=dbank[:, at:at + C],
+                            lhsT=wa_words[j][:, 1024 * ee + 2 * P * b:1024 * ee + 2 * P * (b + 1)].bitcast(FP4X4),
+                            lhsT_scale=was[:, e, P * b:P * (b + 1)],
+                            rhs=hc[:, slots].bitcast(FP8X4), rhs_scale=hs[:, slots], start=True, stop=True)
+                for b in (2 * bb, 2 * bb + 1):
+                    at = 2 * C * (b % 2)
+                    nc.scalar.copy(out=dx[b][:, 2 * C * j:2 * C * (j + 1)], in_=dbank[:, at:at + 2 * C])
+
+        wc = [sb([P, K], U32, "wc%d" % s) for s in range(PASSES)]
+        ws = [sb([P, K], U8, "ws%d" % s) for s in range(PASSES)]
+        for q in range(4):
+            s, half = divmod(q, 2)
+            wb16 = sb([P, K // 2, 4], BF16, "wb16%d" % q)
+            nc.vector.tensor_copy(
+                out=wb16[:].rearrange("p (c i) j -> p c j i", i=4),
+                in_=wraw[q][:].rearrange("p (j c i) -> p c j i", j=4, i=4))
+            cols = slice(256 * half, 256 * (half + 1))
+            nc.vector.quantize_mx(out=wc[s][:, cols].bitcast(FP8X4), scales=ws[s][:, cols],
+                                  in_=wb16[:].rearrange("p c j -> p (c j)"))
+
+        base = sb([P, 4, T], F32, "base")
+        for half in range(2):
+            toks = slice(256 * half, 256 * (half + 1))
+            for bb in range(2):
+                bbank = bank("w", 2, "bbank%d%d" % (half, bb))
+                for i in range(2):
+                    cols = slice(P * (2 * bb + i), P * (2 * bb + i + 1))
+                    for s in range(PASSES):
+                        nc.tensor.matmul_mx(
+                            out=bbank[:, 256 * i:256 * (i + 1)],
+                            lhsT=wc[s][:, cols].bitcast(FP8X4), lhsT_scale=ws[s][:, cols],
+                            rhs=dyw[s][:, toks].bitcast(FP8X4), rhs_scale=dys[:, s, toks],
+                            start=(s == 0), stop=(s == PASSES - 1))
+                to = base[:, 2 * bb:2 * bb + 2, toks]
+                sums = bbank[:].rearrange("p (b c) -> p b c", b=2)
+                if half == 0:
+                    nc.vector.tensor_copy(out=to, in_=sums)
+                else:
+                    nc.scalar.copy(out=to, in_=sums)
+
+        yc = sb([P, T], U32, "yc")
+        ys = sb([P, T], U8, "ys")
+        out_rows = out_0.rearrange("(b p) t -> p b t", p=P)
+        out_words = out_1[0].rearrange("p t d -> p (t d)").bitcast(I32)
+        for t0, t1 in ((0, 256), (256, 384), (384, 512)):
+            n = t1 - t0
+            part = sb([P, 4, n], F32, "part%d" % t0)
+            y = sb([P, 4, n], F32, "y%d" % t0)
+            cut = slice(t0 // 16, t1 // 16)
+            for b in range(4):
+                nc.vector.tensor_tensor(part[:, b, :], dx[b][:].indirect(pos1_sb[:, cut]), base[:, b, t0:t1], ADD)
+            for b in range(4):
+                nc.vector.tensor_tensor(y[:, b, :], dx[b][:].indirect(pos2_sb[:, cut]), part[:, b, :], ADD)
+            nc.sync.dma_start(out=out_rows[:, :, t0:t1], in_=y[:])
+            xbank = bank("w", 2, "xbank%d" % t0)
+            for x in range(n // P):
+                yt = sb([P, K], BF16, "yt%d%d" % (t0, x))
+                for b0, b1 in (((0, 3), (3, 4)) if t1 == T else ((0, 4),)):
+                    tbank = bank("d", 3, "tbank%d%d%d" % (t0, x, b0))
+                    for b in range(b0, b1):
+                        nc.tensor.transpose(tbank[:, P * (b - b0):P * (b - b0 + 1)], y[:, b, P * x:P * (x + 1)],
+                                            ident[:])
+                    nc.scalar.copy(
+                        out=yt[:].rearrange("c (u p h) -> c u p h", u=2, h=2)[:, :, 32 * b0:32 * b1, :],
+                        in_=tbank[:, 0:P * (b1 - b0)].rearrange("c (p u h) -> c u p h", u=2, h=2))
+                words = yt[:].bitcast(F32)
+                for u in range(2):
+                    at = P * (2 * x + u)
+                    nc.tensor.transpose(xbank[:, at:at + P], words[:, P * u:P * (u + 1)], ident[:])
+            yb = sb([P, 4 * n], BF16, "yb%d" % t0)
+            nc.scalar.copy(
+                out=yb[:].bitcast(F32).rearrange("p (x c u) -> p x c u", c=P, u=2),
+                in_=xbank[:, 0:2 * n].rearrange("p (x u c) -> p x c u", c=P, u=2))
+            nc.vector.quantize_mx(out=yc[:, t0:t1].bitcast(FP8X4), scales=ys[:, t0:t1], in_=yb[:])
+            nc.sync.dma_start(out=out_words[:, t0:t1], in_=yc[:, t0:t1].bitcast(I32))
+        for q in range(4):
+            eng = nc.sync if q % 2 == 0 else nc.scalar
+            eng.dma_start(out=out_2[0, 4 * q:4 * q + 4, :].bitcast(I32), in_=ys[32 * q:32 * q + 4, :].bitcast(I32))

@@ -34,225 +34,262 @@ def tile_moe_adb_none_kernel(
         def sb(shape, dtype, name):
             return keep.tile(shape, dtype, name=name, align_bytes=64)
 
-        def bank(tag, bufs, name):
-            return psum.tile([P, 512], F32, name=name, tag=tag, bufs=bufs)
+        def bank(number, name):
+            return psum.tile([P, 512], F32, name=name, offset=2048 * number)
 
         offs_sb = keep.tile([P, S // 16], U16, name="offs_sb")
         pos1_sb = keep.tile([P, T // 16], U16, name="pos1_sb")
         pos2_sb = keep.tile([P, T // 16], U16, name="pos2_sb")
-        dyw_all = sb([P, PASSES * T], I32, "dyw_all")
-        dyw = [dyw_all[:, T * s:T * (s + 1)] for s in range(PASSES)]
+        dyw = [sb([P, T], I32, "dyw%d" % s)[:] for s in range(PASSES)]
         dys = sb([P, PASSES, T], U8, "dys")
-        wbs0 = sb([P, 2 * PASSES, H], U8, "wbs0")
-        wbs1 = sb([P, (E - 2) * PASSES, H], U8, "wbs1")
-        was = sb([P, E, K], U8, "was")
-        blank = laid.tile([P, P], F32, name="blank", align_bytes=64, offset=65536 - 256)
-        wbw0 = sb([P, 4096], U8, "wbw0")
         ident = sb([P, P], F32, "ident")
-        grow_area = laid.tile([P, 8192 + 1280], F32, name="grow_area", align_bytes=64, offset=16384)
-        grow = grow_area[:, 0:P]
         gcol = sb([P, E], F32, "gcol")
+        blank = laid.tile([P, 3072], F32, name="blank", align_bytes=64, offset=0)
+        grow = laid.tile([P, 13312], F32, name="grow", align_bytes=64, offset=12288)
 
+        nc.gpsimd.memset(grow[:, 0:P], 0.0)
         nc.gpsimd.memset(dys[:].bitcast(I32), 0)
-        nc.gpsimd.memset(grow, 0.0)
-        nc.gpsimd.memset(blank[:], 0.0)
-        nc.gpsimd.affine_select(out=ident[:], in_=blank[:], compare_op=mybir.AluOpType.not_equal, fill=1.0,
+        nc.gpsimd.memset(blank[:, 0:P], 0.0)
+        nc.vector.memset(blank[:, P:P + 513].bitcast(I32), 0)
+        nc.vector.memset(grow[:, P:P + 1537].bitcast(I32), 0)
+        nc.gpsimd.affine_select(out=ident[:], in_=blank[:, 0:P], compare_op=mybir.AluOpType.not_equal, fill=1.0,
                                 base=0, pattern=[[-1, P]], channel_multiplier=1)
-        nc.vector.memset(wbs0[:].bitcast(I32), 0)
-        nc.vector.memset(wbs1[:].bitcast(I32), 0)
-        nc.vector.memset(was[:].bitcast(I32), 0)
+        nc.gpsimd.memset(grow[:, P + 1552:P + 2576].bitcast(I32), 0)
+        wbs = [laid.tile([P, 2 * PASSES, H], U8, name="wbs0", align_bytes=64, offset=512),
+               laid.tile([P, (E - 2) * PASSES, H], U8, name="wbs1", align_bytes=64, offset=12288 + 512)]
+        was = laid.tile([P, E, K], U8, name="was", align_bytes=64, offset=12288 + 512 + 6144 + 64)
 
-        def load_scales(eng, plane, rows):
+        def load_scales(plane, rows):
             for r in range(4):
-                eng.dma_start(out=plane[r:P:32].bitcast(I32), in_=rows[r].bitcast(I32))
+                nc.sync.dma_start(out=plane[r:P:32].bitcast(I32), in_=rows[r].bitcast(I32))
 
-        nc.sync.dma_start(offs_sb[:], offs)
-        nc.sync.dma_start(out=dyw_all[:].rearrange("p (s t) -> p s t", s=PASSES),
-                          in_=dy_words.rearrange("s p t d -> p s (t d)").bitcast(I32))
-        nc.sync.dma_start(pos1_sb[:], pos1)
-        nc.sync.dma_start(pos2_sb[:], pos2)
-        nc.sync.dma_start(out=wbw0[:].bitcast(I32).rearrange("p (x c) -> p x c", x=4),
-                          in_=wbt_words[0:2].rearrange("e s p c -> p (e s) c").bitcast(I32))
-        load_scales(nc.sync, dys, dy_scales.rearrange("s (q r) t -> r q s t", r=4))
-        nc.sync.dma_start(out=grow_area[0:E, 0:P], in_=gate[0:1, :].rearrange("o (e u) -> (o e) u", u=C))
-        load_scales(nc.sync, wbs0, wbt_scales[0:2].rearrange("e s (q r) c -> r q (e s) c", r=4))
-        gbank = bank("w", 2, "gbank")
-        nc.tensor.transpose(gbank[:, 0:P], grow, ident[:])
-        nc.scalar.activation(out=gcol[:], in_=gbank[:, 0:E], func=COPY)
+        def late(shape, dtype, name, place):
+            return laid.tile(shape, dtype, name=name, align_bytes=64, offset=4096 * place)
 
-        wraw = [laid.tile([P, 1024], F32, name="wraw%d" % q, align_bytes=64, offset=32768 + 4096 * q)
-                for q in range(4)]
-        wbw1 = laid.tile([P, 4096], U8, name="wbw1", align_bytes=64, offset=65536)
-        wb_words = [wbw0[:], wbw1[:]] + [
-            laid.tile([P, 4096], U8, name="wbw%d" % j, align_bytes=64, offset=16384 + 4096 * (j - 2))[:]
-            for j in (2, 3)]
-        wa_words = [laid.tile([P, 2048], U8, name="waw%d" % j, align_bytes=64, offset=24576 + 2048 * j)[:]
-                    for j in range(PAIRS)]
+        wb_words = [late([P, 4096], U8, "wbw%d" % j, (1, 2, 6, 7)[j]) for j in range(PAIRS)]
+        wa_words = [late([P, 4096], U8, "waw%d" % h, 8 + h) for h in range(2)]
+        spans = ((0, 1), (1, 2), (2, 3), (3, 4))
+        wraw = [late([P, PASSES, 512 * (b1 - b0)], F32, "wraw%d" % b0, 10 + b0) for b0, b1 in spans]
 
         def load_wb(j):
-            nc.sync.dma_start(out=wb_words[j].bitcast(I32).rearrange("p (x c) -> p x c", x=4),
+            nc.sync.dma_start(out=wb_words[j][:].bitcast(I32).rearrange("p (x c) -> p x c", x=4),
                               in_=wbt_words[2 * j:2 * j + 2].rearrange("e s p c -> p (e s) c").bitcast(I32))
 
-        def load_wa(j):
-            nc.sync.dma_start(out=wa_words[j].bitcast(I32).rearrange("p (x c) -> p x c", x=2),
-                              in_=wat_words[2 * j:2 * j + 2].rearrange("e s p c -> p (e s) c").bitcast(I32))
+        def load_wa(h):
+            nc.sync.dma_start(out=wa_words[h][:].bitcast(I32).rearrange("p (e c) -> p e c", e=E),
+                              in_=wat_words[:, 0, :, 512 * h:512 * (h + 1)].rearrange("e p c -> p e c").bitcast(I32))
 
-        def load_wt(q):
-            s, half = divmod(q, 2)
-            rows = wt[512 * s:512 * (s + 1), 256 * half:256 * (half + 1)]
-            nc.sync.dma_start(out=wraw[q][:].rearrange("p (j c) -> p j c", j=4),
-                              in_=rows.rearrange("(p j) c -> p j c", j=4))
+        def load_wt(i):
+            b0, b1 = spans[i]
+            for s in range(PASSES):
+                rows = wt[512 * s:512 * (s + 1), P * b0:P * b1]
+                nc.sync.dma_start(out=wraw[i][:, s, :].rearrange("p (j c) -> p j c", j=4),
+                                  in_=rows.rearrange("(p j) c -> p j c", j=4))
 
+        nc.sync.dma_start(offs_sb[:], offs)
+        nc.sync.dma_start(pos1_sb[:], pos1)
+        nc.sync.dma_start(pos2_sb[:], pos2)
+        nc.sync.dma_start(out=grow[0:E, 0:P], in_=gate[0:1, :].rearrange("o (e u) -> (o e) u", u=C))
+        for s in range(PASSES):
+            nc.sync.dma_start(out=dyw[s], in_=dy_words[s].rearrange("p t d -> p (t d)").bitcast(I32))
+        load_scales(dys, dy_scales.rearrange("s (q r) t -> r q s t", r=4))
+        load_wb(0)
+        load_scales(wbs[0], wbt_scales[0:2].rearrange("e s (q r) c -> r q (e s) c", r=4))
         load_wb(1)
-        load_scales(nc.sync, wbs1, wbt_scales[2:E].rearrange("e s (q r) c -> r q (e s) c", r=4))
-        load_scales(nc.sync, was, wat_scales.rearrange("e s (q r) c -> r q (e s) c", r=4))
-        load_wa(0)
+        load_scales(wbs[1], wbt_scales[2:E].rearrange("e s (q r) c -> r q (e s) c", r=4))
         load_wb(2)
-        load_wa(1)
-        load_wt(0)
         load_wb(3)
+        load_wt(0)
         load_wt(1)
-        load_wa(2)
+        load_scales(was, wat_scales.rearrange("e s (q r) c -> r q (e s) c", r=4))
+        load_wa(0)
         load_wt(2)
+        load_wa(1)
         load_wt(3)
-        load_wa(3)
 
+        gbank = bank(3, "gbank")
+        nc.tensor.transpose(gbank[:, 0:P], grow[:, 0:P], ident[:])
+        nc.scalar.activation(out=gcol[:], in_=gbank[:, 0:E], func=COPY)
+
+        groups = ((0, 2), (2, 4), (4, 6), (6, 7), (7, 8))
         gw = {}
         gs = {}
-
-        def gather(j, s, word_at=None, byte_at=None):
-            if word_at is None:
-                gw[j, s] = sb([P, 2 * C], U32, "gw%d%d" % (j, s))
-                gs[j, s] = sb([P, 2 * C], U8, "gs%d%d" % (j, s))
-            else:
-                gw[j, s] = laid.tile([P, 2 * C], U32, name="gw%d%d" % (j, s), align_bytes=64, offset=word_at)
-                gs[j, s] = laid.tile([P, 2 * C], U8, name="gs%d%d" % (j, s), align_bytes=64, offset=byte_at)
-            cut = offs_sb[:, 16 * j:16 * (j + 1)]
-            nc.vector.tensor_copy(out=gw[j, s][:], in_=dyw[s].bitcast(U32).indirect(cut))
-            nc.vector.tensor_copy(out=gs[j, s][:], in_=dys[:, s, :].indirect(cut))
-
-        dx = [sb([P, S], F32, "dx%d" % b) for b in range(4)]
-
-        gather(0, 0)
-        gather(0, 1)
-        for j in (1, 2):
+        for e0, e1 in groups:
+            n = C * (e1 - e0)
+            cut = offs_sb[:, 8 * e0:8 * e1]
             for s in range(PASSES):
-                at = 49152 + 1280 * (2 * (j - 1) + s)
-                gather(j, s, at, at + 1024)
-        for j in range(PAIRS):
-            wbank = bank("w", 2, "wbank%d" % j)
-            for ee in range(2):
-                e = 2 * j + ee
-                hbank = bank("h", 3, "hbank%d" % e)
-                slots = slice(C * ee, C * (ee + 1))
+                if e0 == 0:
+                    gw[e0, s] = sb([P, n], U32, "gw%d%d" % (e0, s))
+                    gs[e0, s] = sb([P, n], U8, "gs%d%d" % (e0, s))
+                else:
+                    at = 57344 + 1280 * (e0 - 2) + 5 * n * s
+                    gw[e0, s] = laid.tile([P, n], U32, name="gw%d%d" % (e0, s), align_bytes=64, offset=at)
+                    gs[e0, s] = laid.tile([P, n], U8, name="gs%d%d" % (e0, s), align_bytes=64, offset=at + 4 * n)
+                nc.vector.tensor_copy(out=gw[e0, s][:], in_=dyw[s].bitcast(U32).indirect(cut))
+                nc.vector.tensor_copy(out=gs[e0, s][:], in_=dys[:, s, :].indirect(cut))
+
+        hc = {}
+        hs = {}
+        for g, (e0, e1) in enumerate(groups):
+            n = C * (e1 - e0)
+            wbank = bank(4 - g % 2, "wbank%d" % e0)
+            for e in range(e0, e1):
+                hbank = bank(e % 3, "hbank%d" % e)
+                slots = slice(C * (e - e0), C * (e - e0 + 1))
                 for s in range(PASSES):
+                    at = 1024 * (2 * (e % 2) + s)
                     nc.tensor.matmul_mx(
-                        out=hbank[:], lhsT=gw[j, s][:, slots].bitcast(FP8X4), lhsT_scale=gs[j, s][:, slots],
-                        rhs=wb_words[j][:, 1024 * (2 * ee + s):1024 * (2 * ee + s + 1)].bitcast(FP4X4),
-                        rhs_scale=(wbs0[:, 2 * e + s, :] if j == 0 else wbs1[:, 2 * e + s - 4, :]),
+                        out=hbank[:], lhsT=gw[e0, s][:, slots].bitcast(FP8X4), lhsT_scale=gs[e0, s][:, slots],
+                        rhs=wb_words[e // 2][:, at:at + 1024].bitcast(FP4X4),
+                        rhs_scale=(wbs[0][:, 2 * e + s, :] if e < 2 else wbs[1][:, 2 * e + s - 4, :]),
                         start=(s == 0), stop=(s == PASSES - 1))
                 dht = sb([P, H], BF16, "dht%d" % e)
-                nc.scalar.activation(
-                    out=dht[:].rearrange("c (u p h) -> c u p h", u=2, h=2),
-                    in_=hbank[:].rearrange("c (p u h) -> c u p h", u=2, h=2),
-                    func=COPY, scale=gcol[:, e:e + 1])
+                for u0, u1 in (((0, 1), (1, 2)) if e == E - 1 else ((0, 2),)):
+                    nc.scalar.activation(
+                        out=dht[:].rearrange("c (u p h) -> c u p h", u=2, h=2)[:, u0:u1],
+                        in_=hbank[:].rearrange("c (p u h) -> c u p h", u=2, h=2)[:, u0:u1],
+                        func=COPY, scale=gcol[:, e:e + 1])
                 words = dht[:].bitcast(F32)
                 for u in range(2):
-                    at = P * (2 * ee + u)
+                    at = P * (2 * (e - e0) + u)
                     nc.tensor.transpose(wbank[:, at:at + P], words[:, P * u:P * (u + 1)], ident[:])
-            dhb = laid.tile([P, 4 * 2 * C], BF16, name="dhb%d" % j, align_bytes=64, offset=4096 * j + 512)
+            dhb = sb([P, 4 * n], BF16, "dhb%d" % e0)
             nc.scalar.copy(
-                out=dhb[:].bitcast(F32).rearrange("p (x c u) -> p x c u", x=2, u=2),
-                in_=wbank[:].rearrange("p (x u c) -> p x c u", x=2, u=2))
-            hc = sb([P, 2 * C], U32, "hc%d" % j)
-            hs = sb([P, 2 * C], U8, "hs%d" % j)
-            nc.vector.quantize_mx(out=hc[:].bitcast(FP8X4), scales=hs[:], in_=dhb[:])
-            if j == 0:
-                gather(3, 0, 0, 1024)
-                gather(3, 1, 1536, 1280)
-            for bb in range(2):
-                dbank = bank("d", 3, "dbank%d%d" % (j, bb))
-                for b in (2 * bb, 2 * bb + 1):
-                    for ee in range(2):
-                        e = 2 * j + ee
-                        at = 2 * C * (b % 2) + C * ee
-                        slots = slice(C * ee, C * (ee + 1))
-                        nc.tensor.matmul_mx(
-                            out=dbank[:, at:at + C],
-                            lhsT=wa_words[j][:, 1024 * ee + 2 * P * b:1024 * ee + 2 * P * (b + 1)].bitcast(FP4X4),
-                            lhsT_scale=was[:, e, P * b:P * (b + 1)],
-                            rhs=hc[:, slots].bitcast(FP8X4), rhs_scale=hs[:, slots], start=True, stop=True)
-                for b in (2 * bb, 2 * bb + 1):
-                    at = 2 * C * (b % 2)
-                    nc.scalar.copy(out=dx[b][:, 2 * C * j:2 * C * (j + 1)], in_=dbank[:, at:at + 2 * C])
+                out=dhb[:].bitcast(F32).rearrange("p (x c u) -> p x c u", c=C, u=2),
+                in_=wbank[:, 0:2 * n].rearrange("p (x u c) -> p x c u", c=C, u=2))
+            codes = sb([P, n], U32, "hc%d" % e0)
+            scales = sb([P, n], U8, "hs%d" % e0)
+            nc.vector.quantize_mx(out=codes[:].bitcast(FP8X4), scales=scales[:], in_=dhb[:])
+            for e in range(e0, e1):
+                hc[e] = codes[:, C * (e - e0):C * (e - e0 + 1)]
+                hs[e] = scales[:, C * (e - e0):C * (e - e0 + 1)]
 
-        wc = [sb([P, K], U32, "wc%d" % s) for s in range(PASSES)]
-        ws = [sb([P, K], U8, "ws%d" % s) for s in range(PASSES)]
-        for q in range(4):
-            s, half = divmod(q, 2)
-            wb16 = sb([P, K // 2, 4], BF16, "wb16%d" % q)
-            nc.vector.tensor_copy(
-                out=wb16[:].rearrange("p (c i) j -> p c j i", i=4),
-                in_=wraw[q][:].rearrange("p (j c i) -> p c j i", j=4, i=4))
-            cols = slice(256 * half, 256 * (half + 1))
-            nc.vector.quantize_mx(out=wc[s][:, cols].bitcast(FP8X4), scales=ws[s][:, cols],
-                                  in_=wb16[:].rearrange("p c j -> p (c j)"))
+        wc = [sb([P, PASSES, P], U32, "wc%d" % b) for b in range(4)]
+        ws = [sb([P, PASSES, P], U8, "ws%d" % b) for b in range(4)]
+        wb16 = [sb([P, 1024], BF16, "wb16%d" % b) for b in range(4)]
 
-        base = sb([P, 4, T], F32, "base")
-        for half in range(2):
-            toks = slice(256 * half, 256 * (half + 1))
-            for bb in range(2):
-                bbank = bank("w", 2, "bbank%d%d" % (half, bb))
-                for i in range(2):
-                    cols = slice(P * (2 * bb + i), P * (2 * bb + i + 1))
-                    for s in range(PASSES):
-                        nc.tensor.matmul_mx(
-                            out=bbank[:, 256 * i:256 * (i + 1)],
-                            lhsT=wc[s][:, cols].bitcast(FP8X4), lhsT_scale=ws[s][:, cols],
-                            rhs=dyw[s][:, toks].bitcast(FP8X4), rhs_scale=dys[:, s, toks],
-                            start=(s == 0), stop=(s == PASSES - 1))
-                to = base[:, 2 * bb:2 * bb + 2, toks]
-                sums = bbank[:].rearrange("p (b c) -> p b c", b=2)
-                if half == 0:
-                    nc.vector.tensor_copy(out=to, in_=sums)
-                else:
-                    nc.scalar.copy(out=to, in_=sums)
+        def round_wt(b, copy):
+            copy(out=wb16[b][:].rearrange("p (s c i j) -> p s c j i", s=PASSES, i=4, j=4),
+                 in_=wraw[b][:].rearrange("p s (j c i) -> p s c j i", j=4, i=4))
 
-        yc = sb([P, T], U32, "yc")
-        ys = sb([P, T], U8, "ys")
-        out_rows = out_0.rearrange("(b p) t -> p b t", p=P)
+        def quantise_wt(b):
+            nc.vector.quantize_mx(out=wc[b][:].rearrange("p s c -> p (s c)").bitcast(FP8X4),
+                                  scales=ws[b][:].rearrange("p s c -> p (s c)"), in_=wb16[b][:])
+
+        dx = [sb([P, S], F32, "dx%d" % b) for b in range(4)]
+        base = [sb([P, T], F32, "base%d" % b) for b in range(4)]
+
+        def adapters(b, e0, e1, number):
+            dbank = bank(number, "dbank%d%d" % (b, e0))
+            for e in range(e0, e1):
+                at = 512 * e + 2 * P * (b % 2)
+                nc.tensor.matmul_mx(
+                    out=dbank[:, C * (e - e0):C * (e - e0 + 1)],
+                    lhsT=wa_words[b // 2][:, at:at + 2 * P].bitcast(FP4X4),
+                    lhsT_scale=was[:, e, P * b:P * (b + 1)],
+                    rhs=hc[e].bitcast(FP8X4), rhs_scale=hs[e], start=True, stop=True)
+            nc.scalar.copy(out=dx[b][:, C * e0:C * e1], in_=dbank[:, 0:C * (e1 - e0)])
+
+        def frozen(b, number):
+            bbank = bank(number, "bbank%d" % b)
+            for s in range(PASSES):
+                nc.tensor.matmul_mx(
+                    out=bbank[:], lhsT=wc[b][:, s, :].bitcast(FP8X4), lhsT_scale=ws[b][:, s, :],
+                    rhs=dyw[s].bitcast(FP8X4), rhs_scale=dys[:, s, :], start=(s == 0), stop=(s == PASSES - 1))
+            nc.scalar.copy(out=base[b][:], in_=bbank[:])
+
+        ys = sb([P, 4, P], U8, "ys")
         out_words = out_1[0].rearrange("p t d -> p (t d)").bitcast(I32)
-        for t0, t1 in ((0, 256), (256, 384), (384, 512)):
-            n = t1 - t0
-            part = sb([P, 4, n], F32, "part%d" % t0)
-            y = sb([P, 4, n], F32, "y%d" % t0)
-            cut = slice(t0 // 16, t1 // 16)
-            for b in range(4):
-                nc.vector.tensor_tensor(part[:, b, :], dx[b][:].indirect(pos1_sb[:, cut]), base[:, b, t0:t1], ADD)
-            for b in range(4):
-                nc.vector.tensor_tensor(y[:, b, :], dx[b][:].indirect(pos2_sb[:, cut]), part[:, b, :], ADD)
-            nc.sync.dma_start(out=out_rows[:, :, t0:t1], in_=y[:])
-            xbank = bank("w", 2, "xbank%d" % t0)
-            for x in range(n // P):
-                yt = sb([P, K], BF16, "yt%d%d" % (t0, x))
-                for b0, b1 in (((0, 3), (3, 4)) if t1 == T else ((0, 4),)):
-                    tbank = bank("d", 3, "tbank%d%d%d" % (t0, x, b0))
-                    for b in range(b0, b1):
-                        nc.tensor.transpose(tbank[:, P * (b - b0):P * (b - b0 + 1)], y[:, b, P * x:P * (x + 1)],
-                                            ident[:])
-                    nc.scalar.copy(
-                        out=yt[:].rearrange("c (u p h) -> c u p h", u=2, h=2)[:, :, 32 * b0:32 * b1, :],
-                        in_=tbank[:, 0:P * (b1 - b0)].rearrange("c (p u h) -> c u p h", u=2, h=2))
-                words = yt[:].bitcast(F32)
-                for u in range(2):
-                    at = P * (2 * x + u)
-                    nc.tensor.transpose(xbank[:, at:at + P], words[:, P * u:P * (u + 1)], ident[:])
-            yb = sb([P, 4 * n], BF16, "yb%d" % t0)
+
+        yt = [sb([P, K], BF16, "yt%d" % b) for b in range(4)]
+
+        yb = [sb([P, 4 * P], BF16, "yb%d" % b) for b in range(4)]
+
+        part = {}
+        y = {}
+
+        def first_slot(b, x0, x1):
+            if (b, x0) == (3, 3):
+                wide = laid.tile([P, T], F32, name="part33", align_bytes=64, offset=65536)
+                part[b, x0] = wide[:, 0:P]
+            else:
+                part[b, x0] = sb([P, P * (x1 - x0)], F32, "part%d%d" % (b, x0))[:]
+            nc.vector.tensor_tensor(part[b, x0], dx[b][:].indirect(pos1_sb[:, 8 * x0:8 * x1]),
+                                    base[b][:, P * x0:P * x1], ADD)
+
+        def second_slot(b, x0, x1):
+            nc.vector.tensor_tensor(y[b][:, P * x0:P * x1], dx[b][:].indirect(pos2_sb[:, 8 * x0:8 * x1]),
+                                    part[b, x0], ADD)
+
+        def turn(b, x0, x1, number):
+            if x1 == 4:
+                nc.sync.dma_start(out=out_0[P * b:P * (b + 1), :], in_=y[b][:])
+            tbank = bank(number, "tbank%d%d" % (b, x0))
+            for x in range(x0, x1):
+                nc.tensor.transpose(tbank[:, P * (x - x0):P * (x - x0 + 1)], y[b][:, P * x:P * (x + 1)], ident[:])
             nc.scalar.copy(
-                out=yb[:].bitcast(F32).rearrange("p (x c u) -> p x c u", c=P, u=2),
-                in_=xbank[:, 0:2 * n].rearrange("p (x u c) -> p x c u", c=P, u=2))
-            nc.vector.quantize_mx(out=yc[:, t0:t1].bitcast(FP8X4), scales=ys[:, t0:t1], in_=yb[:])
-            nc.sync.dma_start(out=out_words[:, t0:t1], in_=yc[:, t0:t1].bitcast(I32))
-        for q in range(4):
-            eng = nc.sync if q % 2 == 0 else nc.scalar
-            eng.dma_start(out=out_2[0, 4 * q:4 * q + 4, :].bitcast(I32), in_=ys[32 * q:32 * q + 4, :].bitcast(I32))
+                out=yt[b][:].rearrange("c (u p h) -> c u p h", u=2, h=2)[:, :, 32 * x0:32 * x1, :],
+                in_=tbank[:, 0:P * (x1 - x0)].rearrange("c (p u h) -> c u p h", u=2, h=2))
+
+        def combine(b, number):
+            y[b] = sb([P, T], F32, "y%d" % b)
+            for x0 in (0, 2):
+                first_slot(b, x0, x0 + 2)
+            for x0 in (0, 2):
+                second_slot(b, x0, x0 + 2)
+            turn(b, 0, 4, number)
+
+        def planes(b, number):
+            xbank = bank(number, "xbank%d" % b)
+            words = yt[b][:].bitcast(F32)
+            for u in range(2):
+                nc.tensor.transpose(xbank[:, P * u:P * (u + 1)], words[:, P * u:P * (u + 1)], ident[:])
+            nc.scalar.copy(out=yb[b][:].bitcast(F32).rearrange("p (c u) -> p c u", u=2),
+                           in_=xbank[:, 0:2 * P].rearrange("p (u c) -> p c u", u=2))
+
+        round_wt(0, nc.vector.tensor_copy)
+        quantise_wt(0)
+        round_wt(1, nc.vector.tensor_copy)
+        quantise_wt(1)
+        adapters(0, 0, 4, 0)
+        frozen(0, 1)
+        adapters(0, 4, 7, 5)
+        adapters(0, 7, 8, 6)
+        round_wt(2, nc.vector.tensor_copy)
+        quantise_wt(2)
+        adapters(1, 0, 4, 1)
+        adapters(1, 4, 8, 5)
+        frozen(1, 6)
+        round_wt(3, nc.scalar.copy)
+        quantise_wt(3)
+        adapters(2, 0, 4, 0)
+        adapters(2, 4, 8, 1)
+        frozen(2, 5)
+        combine(0, 6)
+        adapters(3, 0, 4, 0)
+        adapters(3, 4, 8, 1)
+        planes(0, 5)
+        frozen(3, 6)
+        combine(1, 0)
+        combine(2, 1)
+        planes(1, 5)
+        planes(2, 6)
+        y[3] = sb([P, T], F32, "y3")
+        first_slot(3, 0, 2)
+        first_slot(3, 2, 3)
+        second_slot(3, 0, 2)
+        first_slot(3, 3, 4)
+        second_slot(3, 2, 3)
+        turn(3, 0, 3, 1)
+        second_slot(3, 3, 4)
+        turn(3, 3, 4, 5)
+        planes(3, 0)
+        yc = laid.tile([P, 4, P], U32, name="yc", align_bytes=64, offset=65536)
+        for b in range(4):
+            nc.vector.quantize_mx(out=yc[:, b, :].bitcast(FP8X4), scales=ys[:, b, :], in_=yb[b][:])
+        word_rows = out_words.rearrange("(b q) t -> q b t", b=4)
+        scale_rows = out_2[0].rearrange("(b g) t -> g b t", g=4)
+        for x in range(4):
+            nc.sync.dma_start(out=word_rows[:, :, P * x:P * (x + 1)], in_=yc[32 * x:32 * (x + 1)].bitcast(I32))
+            nc.scalar.dma_start(out=scale_rows[:, :, P * x:P * (x + 1)].bitcast(I32),
+                          in_=ys[32 * x:32 * x + 4].bitcast(I32))

@@ -45,19 +45,21 @@ def tile_moe_adb_none_kernel(
         ident = sb([P, P], F32, "ident")
         gcol = sb([P, E], F32, "gcol")
         blank = laid.tile([P, 3072], F32, name="blank", align_bytes=64, offset=0)
-        grow = laid.tile([P, 13312], F32, name="grow", align_bytes=64, offset=12288)
+        later = laid.tile([P, 5120], F32, name="later", align_bytes=64, offset=12288)
+        grow = laid.tile([P, 10240], F32, name="grow", align_bytes=64, offset=32768)
 
         nc.gpsimd.memset(grow[:, 0:P], 0.0)
         nc.gpsimd.memset(dys[:].bitcast(I32), 0)
-        nc.gpsimd.memset(blank[:, 0:P], 0.0)
+        zeros = sb([P, P], F32, "zeros")
+        nc.gpsimd.memset(zeros[:], 0.0)
         nc.vector.memset(blank[:, P:P + 513].bitcast(I32), 0)
-        nc.vector.memset(grow[:, P:P + 1537].bitcast(I32), 0)
-        nc.gpsimd.affine_select(out=ident[:], in_=blank[:, 0:P], compare_op=mybir.AluOpType.not_equal, fill=1.0,
+        nc.vector.memset(later[:, P:P + 1537].bitcast(I32), 0)
+        nc.gpsimd.affine_select(out=ident[:], in_=zeros[:], compare_op=mybir.AluOpType.not_equal, fill=1.0,
                                 base=0, pattern=[[-1, P]], channel_multiplier=1)
-        nc.gpsimd.memset(grow[:, P + 1552:P + 2576].bitcast(I32), 0)
+        nc.gpsimd.memset(grow[:, 9216:10240].bitcast(I32), 0)
         wbs = [laid.tile([P, 2 * PASSES, H], U8, name="wbs0", align_bytes=64, offset=512),
                laid.tile([P, (E - 2) * PASSES, H], U8, name="wbs1", align_bytes=64, offset=12288 + 512)]
-        was = laid.tile([P, E, K], U8, name="was", align_bytes=64, offset=12288 + 512 + 6144 + 64)
+        was = laid.tile([P, E, K], U8, name="was", align_bytes=64, offset=69632)
 
         def load_scales(plane, rows):
             for r in range(4):

@@ -52,8 +52,10 @@ def tile_moe_adb_none_kernel(
         nc.gpsimd.memset(dys[:].bitcast(I32), 0)
         zeros = sb([P, P], F32, "zeros")
         nc.gpsimd.memset(zeros[:], 0.0)
-        nc.vector.memset(blank[:, P:P + 513].bitcast(I32), 0)
-        nc.vector.memset(later[:, P:P + 1537].bitcast(I32), 0)
+        for w0, w1 in ((0, 255), (255, 512)):
+            nc.vector.memset(blank[:, P + w0:P + w1].bitcast(I32), 0)
+        for w0, w1 in ((0, 767), (767, 1536)):
+            nc.vector.memset(later[:, P + w0:P + w1].bitcast(I32), 0)
         nc.gpsimd.affine_select(out=ident[:], in_=zeros[:], compare_op=mybir.AluOpType.not_equal, fill=1.0,
                                 base=0, pattern=[[-1, P]], channel_multiplier=1)
         nc.gpsimd.memset(grow[:, 9216:10240].bitcast(I32), 0)
@@ -275,6 +277,12 @@ def tile_moe_adb_none_kernel(
         combine(1, 0)
         combine(2, 1)
         planes(1, 5)
+        warm = bank(0, "warm")
+        for s in range(PASSES):
+            nc.tensor.matmul_mx(
+                out=warm[:], lhsT=wc[0][:, s, :].bitcast(FP8X4), lhsT_scale=ws[0][:, s, :],
+                rhs=wb_words[0][:, 1024 * s:1024 * (s + 1)].bitcast(FP4X4), rhs_scale=wbs[0][:, s, :],
+                start=(s == 0), stop=(s == PASSES - 1))
         planes(2, 6)
         y[3] = sb([P, T], F32, "y3")
         first_slot(3, 0, 2)

@@ -5,8 +5,9 @@ import concourse.mybir as mybir
 K, T, E, C, H, N = 512, 512, 8, 128, 512, 1024
 S = E * C
 P = 128
-PASSES = 2
+PASSES = N // 512
 PAIRS = E // 2
+BLOCKS = K // P
 FLOPS = 2 * N * K * T + 2 * N * H * S + 2 * H * K * S
 
 F32 = mybir.dt.float32
@@ -19,6 +20,19 @@ FP8X4 = mybir.dt.float8_e4m3fn_x4
 FP4X4 = mybir.dt.float4_e2m1fn_x4
 COPY = mybir.ActivationFunctionType.Copy
 ADD = mybir.AluOpType.add
+
+FIRST_AREA = 0
+SECOND_AREA = 12288
+LATE_AREA = 32768
+PLANE_AT = 512
+WB_WORDS_AT = (4096, 8192, 24576, 28672)
+WA_WORDS_AT = 32768
+WT_AT = 40960
+GATHERED_AT = 57344
+CODES_AT = 65536
+WA_PLANE_AT = 69632
+
+GROUPS = ((0, 2), (2, 4), (4, 6), (6, 7), (7, 8))
 
 
 def tile_moe_adb_none_kernel(
@@ -34,6 +48,9 @@ def tile_moe_adb_none_kernel(
         def sb(shape, dtype, name):
             return keep.tile(shape, dtype, name=name, align_bytes=64)
 
+        def place(shape, dtype, name, offset):
+            return laid.tile(shape, dtype, name=name, align_bytes=64, offset=offset)
+
         def bank(number, name):
             return psum.tile([P, 512], F32, name=name, offset=2048 * number)
 
@@ -44,36 +61,37 @@ def tile_moe_adb_none_kernel(
         dys = sb([P, PASSES, T], U8, "dys")
         ident = sb([P, P], F32, "ident")
         gcol = sb([P, E], F32, "gcol")
-        blank = laid.tile([P, 3072], F32, name="blank", align_bytes=64, offset=0)
-        later = laid.tile([P, 5120], F32, name="later", align_bytes=64, offset=12288)
-        grow = laid.tile([P, 10240], F32, name="grow", align_bytes=64, offset=32768)
+        first_area = place([P, 3072], F32, "first_area", FIRST_AREA)
+        second_area = place([P, 5120], F32, "second_area", SECOND_AREA)
+        late_area = place([P, 10240], F32, "late_area", LATE_AREA)
+        gate_rows = late_area[:, 0:P]
 
-        nc.gpsimd.memset(grow[:, 0:P], 0.0)
+        def clear_plane(area, words):
+            start = PLANE_AT // 4
+            cut = words // 2 - 1
+            for w0, w1 in ((0, cut), (cut, words)):
+                nc.vector.memset(area[:, start + w0:start + w1].bitcast(I32), 0)
+
+        nc.gpsimd.memset(gate_rows, 0.0)
         nc.gpsimd.memset(dys[:].bitcast(I32), 0)
         zeros = sb([P, P], F32, "zeros")
         nc.gpsimd.memset(zeros[:], 0.0)
-        for w0, w1 in ((0, 255), (255, 512)):
-            nc.vector.memset(blank[:, P + w0:P + w1].bitcast(I32), 0)
-        for w0, w1 in ((0, 767), (767, 1536)):
-            nc.vector.memset(later[:, P + w0:P + w1].bitcast(I32), 0)
+        clear_plane(first_area, 2 * PASSES * H // 4)
+        clear_plane(second_area, (E - 2) * PASSES * H // 4)
         nc.gpsimd.affine_select(out=ident[:], in_=zeros[:], compare_op=mybir.AluOpType.not_equal, fill=1.0,
                                 base=0, pattern=[[-1, P]], channel_multiplier=1)
-        nc.gpsimd.memset(grow[:, 9216:10240].bitcast(I32), 0)
-        wbs = [laid.tile([P, 2 * PASSES, H], U8, name="wbs0", align_bytes=64, offset=512),
-               laid.tile([P, (E - 2) * PASSES, H], U8, name="wbs1", align_bytes=64, offset=12288 + 512)]
-        was = laid.tile([P, E, K], U8, name="was", align_bytes=64, offset=69632)
+        wa_plane_word = (WA_PLANE_AT - LATE_AREA) // 4
+        nc.gpsimd.memset(late_area[:, wa_plane_word:wa_plane_word + E * K // 4].bitcast(I32), 0)
+        wbs = [place([P, 2 * PASSES, H], U8, "wbs0", FIRST_AREA + PLANE_AT),
+               place([P, (E - 2) * PASSES, H], U8, "wbs1", SECOND_AREA + PLANE_AT)]
+        was = place([P, E, K], U8, "was", WA_PLANE_AT)
+        wb_words = [place([P, 4096], U8, "wbw%d" % j, WB_WORDS_AT[j]) for j in range(PAIRS)]
+        wa_words = [place([P, 4096], U8, "waw%d" % h, WA_WORDS_AT + 4096 * h) for h in range(2)]
+        wraw = [place([P, PASSES, 512], F32, "wraw%d" % b, WT_AT + 4096 * b) for b in range(BLOCKS)]
 
         def load_scales(plane, rows):
             for r in range(4):
                 nc.sync.dma_start(out=plane[r:P:32].bitcast(I32), in_=rows[r].bitcast(I32))
-
-        def late(shape, dtype, name, place):
-            return laid.tile(shape, dtype, name=name, align_bytes=64, offset=4096 * place)
-
-        wb_words = [late([P, 4096], U8, "wbw%d" % j, (1, 2, 6, 7)[j]) for j in range(PAIRS)]
-        wa_words = [late([P, 4096], U8, "waw%d" % h, 8 + h) for h in range(2)]
-        spans = ((0, 1), (1, 2), (2, 3), (3, 4))
-        wraw = [late([P, PASSES, 512 * (b1 - b0)], F32, "wraw%d" % b0, 10 + b0) for b0, b1 in spans]
 
         def load_wb(j):
             nc.sync.dma_start(out=wb_words[j][:].bitcast(I32).rearrange("p (x c) -> p x c", x=4),
@@ -83,17 +101,16 @@ def tile_moe_adb_none_kernel(
             nc.sync.dma_start(out=wa_words[h][:].bitcast(I32).rearrange("p (e c) -> p e c", e=E),
                               in_=wat_words[:, 0, :, 512 * h:512 * (h + 1)].rearrange("e p c -> p e c").bitcast(I32))
 
-        def load_wt(i):
-            b0, b1 = spans[i]
+        def load_wt(b):
             for s in range(PASSES):
-                rows = wt[512 * s:512 * (s + 1), P * b0:P * b1]
-                nc.sync.dma_start(out=wraw[i][:, s, :].rearrange("p (j c) -> p j c", j=4),
+                rows = wt[512 * s:512 * (s + 1), P * b:P * (b + 1)]
+                nc.sync.dma_start(out=wraw[b][:, s, :].rearrange("p (j c) -> p j c", j=4),
                                   in_=rows.rearrange("(p j) c -> p j c", j=4))
 
         nc.sync.dma_start(offs_sb[:], offs)
         nc.sync.dma_start(pos1_sb[:], pos1)
         nc.sync.dma_start(pos2_sb[:], pos2)
-        nc.sync.dma_start(out=grow[0:E, 0:P], in_=gate[0:1, :].rearrange("o (e u) -> (o e) u", u=C))
+        nc.sync.dma_start(out=late_area[0:E, 0:P], in_=gate[0:1, :].rearrange("o (e u) -> (o e) u", u=C))
         for s in range(PASSES):
             nc.sync.dma_start(out=dyw[s], in_=dy_words[s].rearrange("p t d -> p (t d)").bitcast(I32))
         load_scales(dys, dy_scales.rearrange("s (q r) t -> r q s t", r=4))
@@ -112,13 +129,12 @@ def tile_moe_adb_none_kernel(
         load_wt(3)
 
         gbank = bank(3, "gbank")
-        nc.tensor.transpose(gbank[:, 0:P], grow[:, 0:P], ident[:])
+        nc.tensor.transpose(gbank[:, 0:P], gate_rows, ident[:])
         nc.scalar.activation(out=gcol[:], in_=gbank[:, 0:E], func=COPY)
 
-        groups = ((0, 2), (2, 4), (4, 6), (6, 7), (7, 8))
         gw = {}
         gs = {}
-        for e0, e1 in groups:
+        for e0, e1 in GROUPS:
             n = C * (e1 - e0)
             cut = offs_sb[:, 8 * e0:8 * e1]
             for s in range(PASSES):
@@ -126,15 +142,15 @@ def tile_moe_adb_none_kernel(
                     gw[e0, s] = sb([P, n], U32, "gw%d%d" % (e0, s))
                     gs[e0, s] = sb([P, n], U8, "gs%d%d" % (e0, s))
                 else:
-                    at = 57344 + 1280 * (e0 - 2) + 5 * n * s
-                    gw[e0, s] = laid.tile([P, n], U32, name="gw%d%d" % (e0, s), align_bytes=64, offset=at)
-                    gs[e0, s] = laid.tile([P, n], U8, name="gs%d%d" % (e0, s), align_bytes=64, offset=at + 4 * n)
+                    at = GATHERED_AT + 5 * (C * PASSES * (e0 - 2) + n * s)
+                    gw[e0, s] = place([P, n], U32, "gw%d%d" % (e0, s), at)
+                    gs[e0, s] = place([P, n], U8, "gs%d%d" % (e0, s), at + 4 * n)
                 nc.vector.tensor_copy(out=gw[e0, s][:], in_=dyw[s].bitcast(U32).indirect(cut))
                 nc.vector.tensor_copy(out=gs[e0, s][:], in_=dys[:, s, :].indirect(cut))
 
         hc = {}
         hs = {}
-        for g, (e0, e1) in enumerate(groups):
+        for g, (e0, e1) in enumerate(GROUPS):
             n = C * (e1 - e0)
             wbank = bank(4 - g % 2, "wbank%d" % e0)
             for e in range(e0, e1):
@@ -145,7 +161,7 @@ def tile_moe_adb_none_kernel(
                     nc.tensor.matmul_mx(
                         out=hbank[:], lhsT=gw[e0, s][:, slots].bitcast(FP8X4), lhsT_scale=gs[e0, s][:, slots],
                         rhs=wb_words[e // 2][:, at:at + 1024].bitcast(FP4X4),
-                        rhs_scale=(wbs[0][:, 2 * e + s, :] if e < 2 else wbs[1][:, 2 * e + s - 4, :]),
+                        rhs_scale=(wbs[0][:, 2 * e + s, :] if e < 2 else wbs[1][:, 2 * (e - 2) + s, :]),
                         start=(s == 0), stop=(s == PASSES - 1))
                 dht = sb([P, H], BF16, "dht%d" % e)
                 for u0, u1 in (((0, 1), (1, 2)) if e == E - 1 else ((0, 2),)):
@@ -153,10 +169,10 @@ def tile_moe_adb_none_kernel(
                         out=dht[:].rearrange("c (u p h) -> c u p h", u=2, h=2)[:, u0:u1],
                         in_=hbank[:].rearrange("c (p u h) -> c u p h", u=2, h=2)[:, u0:u1],
                         func=COPY, scale=gcol[:, e:e + 1])
-                words = dht[:].bitcast(F32)
+                pairs = dht[:].bitcast(F32)
                 for u in range(2):
                     at = P * (2 * (e - e0) + u)
-                    nc.tensor.transpose(wbank[:, at:at + P], words[:, P * u:P * (u + 1)], ident[:])
+                    nc.tensor.transpose(wbank[:, at:at + P], pairs[:, P * u:P * (u + 1)], ident[:])
             dhb = sb([P, 4 * n], BF16, "dhb%d" % e0)
             nc.scalar.copy(
                 out=dhb[:].bitcast(F32).rearrange("p (x c u) -> p x c u", c=C, u=2),
@@ -168,20 +184,18 @@ def tile_moe_adb_none_kernel(
                 hc[e] = codes[:, C * (e - e0):C * (e - e0 + 1)]
                 hs[e] = scales[:, C * (e - e0):C * (e - e0 + 1)]
 
-        wc = [sb([P, PASSES, P], U32, "wc%d" % b) for b in range(4)]
-        ws = [sb([P, PASSES, P], U8, "ws%d" % b) for b in range(4)]
-        wb16 = [sb([P, 1024], BF16, "wb16%d" % b) for b in range(4)]
+        wc = [sb([P, PASSES, P], U32, "wc%d" % b) for b in range(BLOCKS)]
+        ws = [sb([P, PASSES, P], U8, "ws%d" % b) for b in range(BLOCKS)]
+        wt16 = [sb([P, PASSES * 512], BF16, "wt16%d" % b) for b in range(BLOCKS)]
 
-        def round_wt(b, copy):
-            copy(out=wb16[b][:].rearrange("p (s c i j) -> p s c j i", s=PASSES, i=4, j=4),
+        def quantise_wt(b, copy):
+            copy(out=wt16[b][:].rearrange("p (s c i j) -> p s c j i", s=PASSES, i=4, j=4),
                  in_=wraw[b][:].rearrange("p s (j c i) -> p s c j i", j=4, i=4))
-
-        def quantise_wt(b):
             nc.vector.quantize_mx(out=wc[b][:].rearrange("p s c -> p (s c)").bitcast(FP8X4),
-                                  scales=ws[b][:].rearrange("p s c -> p (s c)"), in_=wb16[b][:])
+                                  scales=ws[b][:].rearrange("p s c -> p (s c)"), in_=wt16[b][:])
 
-        dx = [sb([P, S], F32, "dx%d" % b) for b in range(4)]
-        base = [sb([P, T], F32, "base%d" % b) for b in range(4)]
+        dx = [sb([P, S], F32, "dx%d" % b) for b in range(BLOCKS)]
+        base = [sb([P, T], F32, "base%d" % b) for b in range(BLOCKS)]
 
         def adapters(b, e0, e1, number):
             dbank = bank(number, "dbank%d%d" % (b, e0))
@@ -202,20 +216,17 @@ def tile_moe_adb_none_kernel(
                     rhs=dyw[s].bitcast(FP8X4), rhs_scale=dys[:, s, :], start=(s == 0), stop=(s == PASSES - 1))
             nc.scalar.copy(out=base[b][:], in_=bbank[:])
 
-        ys = sb([P, 4, P], U8, "ys")
-        out_words = out_1[0].rearrange("p t d -> p (t d)").bitcast(I32)
-
-        yt = [sb([P, K], BF16, "yt%d" % b) for b in range(4)]
-
-        yb = [sb([P, 4 * P], BF16, "yb%d" % b) for b in range(4)]
-
+        ys = sb([P, BLOCKS, P], U8, "ys")
+        yt = [sb([P, K], BF16, "yt%d" % b) for b in range(BLOCKS)]
+        yb = [sb([P, 4 * P], BF16, "yb%d" % b) for b in range(BLOCKS)]
         part = {}
         y = {}
+        last = BLOCKS - 1
 
         def first_slot(b, x0, x1):
-            if (b, x0) == (3, 3):
-                wide = laid.tile([P, T], F32, name="part33", align_bytes=64, offset=65536)
-                part[b, x0] = wide[:, 0:P]
+            if (b, x0) == (last, last):
+                under_codes = place([P, T], F32, "part33", CODES_AT)
+                part[b, x0] = under_codes[:, 0:P]
             else:
                 part[b, x0] = sb([P, P * (x1 - x0)], F32, "part%d%d" % (b, x0))[:]
             nc.vector.tensor_tensor(part[b, x0], dx[b][:].indirect(pos1_sb[:, 8 * x0:8 * x1]),
@@ -243,63 +254,54 @@ def tile_moe_adb_none_kernel(
                 second_slot(b, x0, x0 + 2)
             turn(b, 0, 4, number)
 
-        def planes(b, number):
+        def weave(b, number):
             xbank = bank(number, "xbank%d" % b)
-            words = yt[b][:].bitcast(F32)
+            pairs = yt[b][:].bitcast(F32)
             for u in range(2):
-                nc.tensor.transpose(xbank[:, P * u:P * (u + 1)], words[:, P * u:P * (u + 1)], ident[:])
+                nc.tensor.transpose(xbank[:, P * u:P * (u + 1)], pairs[:, P * u:P * (u + 1)], ident[:])
             nc.scalar.copy(out=yb[b][:].bitcast(F32).rearrange("p (c u) -> p c u", u=2),
                            in_=xbank[:, 0:2 * P].rearrange("p (u c) -> p c u", u=2))
 
-        round_wt(0, nc.vector.tensor_copy)
-        quantise_wt(0)
-        round_wt(1, nc.vector.tensor_copy)
-        quantise_wt(1)
+        quantise_wt(0, nc.vector.tensor_copy)
+        quantise_wt(1, nc.vector.tensor_copy)
         adapters(0, 0, 4, 0)
         frozen(0, 1)
         adapters(0, 4, 7, 5)
         adapters(0, 7, 8, 6)
-        round_wt(2, nc.vector.tensor_copy)
-        quantise_wt(2)
+        quantise_wt(2, nc.vector.tensor_copy)
         adapters(1, 0, 4, 1)
         adapters(1, 4, 8, 5)
         frozen(1, 6)
-        round_wt(3, nc.scalar.copy)
-        quantise_wt(3)
+        quantise_wt(3, nc.scalar.copy)
         adapters(2, 0, 4, 0)
         adapters(2, 4, 8, 1)
         frozen(2, 5)
         combine(0, 6)
         adapters(3, 0, 4, 0)
         adapters(3, 4, 8, 1)
-        planes(0, 5)
+        weave(0, 5)
         frozen(3, 6)
         combine(1, 0)
         combine(2, 1)
-        planes(1, 5)
-        warm = bank(0, "warm")
-        for s in range(PASSES):
-            nc.tensor.matmul_mx(
-                out=warm[:], lhsT=wc[0][:, s, :].bitcast(FP8X4), lhsT_scale=ws[0][:, s, :],
-                rhs=wb_words[0][:, 1024 * s:1024 * (s + 1)].bitcast(FP4X4), rhs_scale=wbs[0][:, s, :],
-                start=(s == 0), stop=(s == PASSES - 1))
-        planes(2, 6)
-        y[3] = sb([P, T], F32, "y3")
-        first_slot(3, 0, 2)
-        first_slot(3, 2, 3)
-        second_slot(3, 0, 2)
-        first_slot(3, 3, 4)
-        second_slot(3, 2, 3)
-        turn(3, 0, 3, 1)
-        second_slot(3, 3, 4)
-        turn(3, 3, 4, 5)
-        planes(3, 0)
-        yc = laid.tile([P, 4, P], U32, name="yc", align_bytes=64, offset=65536)
-        for b in range(4):
+        weave(1, 5)
+        weave(2, 6)
+        y[last] = sb([P, T], F32, "y3")
+        first_slot(last, 0, 2)
+        first_slot(last, 2, 3)
+        second_slot(last, 0, 2)
+        first_slot(last, 3, 4)
+        second_slot(last, 2, 3)
+        turn(last, 0, 3, 1)
+        second_slot(last, 3, 4)
+        turn(last, 3, 4, 5)
+        weave(last, 0)
+
+        yc = place([P, BLOCKS, P], U32, "yc", CODES_AT)
+        for b in range(BLOCKS):
             nc.vector.quantize_mx(out=yc[:, b, :].bitcast(FP8X4), scales=ys[:, b, :], in_=yb[b][:])
-        word_rows = out_words.rearrange("(b q) t -> q b t", b=4)
+        word_rows = out_1[0].rearrange("p t d -> p (t d)").bitcast(I32).rearrange("(b q) t -> q b t", b=BLOCKS)
         scale_rows = out_2[0].rearrange("(b g) t -> g b t", g=4)
         for x in range(4):
             nc.sync.dma_start(out=word_rows[:, :, P * x:P * (x + 1)], in_=yc[32 * x:32 * (x + 1)].bitcast(I32))
             nc.scalar.dma_start(out=scale_rows[:, :, P * x:P * (x + 1)].bitcast(I32),
-                          in_=ys[32 * x:32 * x + 4].bitcast(I32))
+                                in_=ys[32 * x:32 * x + 4].bitcast(I32))

@@ -26,11 +26,12 @@ SECOND_AREA = 12288
 LATE_AREA = 32768
 PLANE_AT = 512
 WB_WORDS_AT = (4096, 8192, 24576, 28672)
-WA_WORDS_AT = 32768
-WT_AT = 40960
-GATHERED_AT = 57344
-CODES_AT = 65536
-WA_PLANE_AT = 69632
+WA_WORDS_AT = 40960
+WT_AT = (49152, 53248, 57344, 61440)
+SECOND_AT = 65536
+GATHERED_AT = 90112
+WT16_AT = 98304
+BOTH_AT = 81920
 
 GROUPS = ((0, 2), (2, 4), (4, 6), (6, 7), (7, 8))
 
@@ -61,33 +62,41 @@ def tile_moe_adb_none_kernel(
         dys = sb([P, PASSES, T], U8, "dys")
         ident = sb([P, P], F32, "ident")
         gcol = sb([P, E], F32, "gcol")
+        gate_rows = place([P, 1920], F32, "gate_area", GATHERED_AT)[:, 0:P]
         first_area = place([P, 3072], F32, "first_area", FIRST_AREA)
         second_area = place([P, 5120], F32, "second_area", SECOND_AREA)
-        late_area = place([P, 10240], F32, "late_area", LATE_AREA)
-        gate_rows = late_area[:, 0:P]
+        late_area = place([P, 8192], F32, "late_area", LATE_AREA)
 
-        def clear_plane(area, words):
-            start = PLANE_AT // 4
+        def clear_on_vector(area, start, words):
             cut = words // 2 - 1
             for w0, w1 in ((0, cut), (cut, words)):
                 nc.vector.memset(area[:, start + w0:start + w1].bitcast(I32), 0)
 
-        nc.gpsimd.memset(gate_rows, 0.0)
+        def clear_on_scalar(area, start, words):
+            nc.scalar.copy(out=area[:, start:start + words].bitcast(U32).rearrange("p (a c) -> p a c", c=P),
+                           in_=zeros[:].bitcast(U32).unsqueeze(1).to_broadcast([P, words // P, P]))
+
+        plane = PLANE_AT // 4
         nc.gpsimd.memset(dys[:].bitcast(I32), 0)
+        nc.gpsimd.memset(gate_rows, 0.0)
         zeros = sb([P, P], F32, "zeros")
         nc.gpsimd.memset(zeros[:], 0.0)
-        clear_plane(first_area, 2 * PASSES * H // 4)
-        clear_plane(second_area, (E - 2) * PASSES * H // 4)
+        clear_on_vector(first_area, plane, 512)
+        clear_on_vector(second_area, plane, 512)
         nc.gpsimd.affine_select(out=ident[:], in_=zeros[:], compare_op=mybir.AluOpType.not_equal, fill=1.0,
                                 base=0, pattern=[[-1, P]], channel_multiplier=1)
-        wa_plane_word = (WA_PLANE_AT - LATE_AREA) // 4
-        nc.gpsimd.memset(late_area[:, wa_plane_word:wa_plane_word + E * K // 4].bitcast(I32), 0)
+        nc.gpsimd.memset(second_area[:, plane + 512:plane + 1024].bitcast(I32), 0)
+        clear_on_scalar(second_area, plane + 1024, 512)
+        clear_on_scalar(late_area, plane, 1024)
         wbs = [place([P, 2 * PASSES, H], U8, "wbs0", FIRST_AREA + PLANE_AT),
                place([P, (E - 2) * PASSES, H], U8, "wbs1", SECOND_AREA + PLANE_AT)]
-        was = place([P, E, K], U8, "was", WA_PLANE_AT)
+        was = place([P, E, K], U8, "was", LATE_AREA + PLANE_AT)
         wb_words = [place([P, 4096], U8, "wbw%d" % j, WB_WORDS_AT[j]) for j in range(PAIRS)]
         wa_words = [place([P, 4096], U8, "waw%d" % h, WA_WORDS_AT + 4096 * h) for h in range(2)]
-        wraw = [place([P, PASSES, 512], F32, "wraw%d" % b, WT_AT + 4096 * b) for b in range(BLOCKS)]
+        wraw = {}
+        for h in range(2):
+            for s in range(PASSES):
+                wraw[h, s] = place([P, 4, 256], F32, "wraw%d%d" % (h, s), WT_AT[2 * h + s])
 
         def load_scales(plane, rows):
             for r in range(4):
@@ -101,34 +110,32 @@ def tile_moe_adb_none_kernel(
             nc.sync.dma_start(out=wa_words[h][:].bitcast(I32).rearrange("p (e c) -> p e c", e=E),
                               in_=wat_words[:, 0, :, 512 * h:512 * (h + 1)].rearrange("e p c -> p e c").bitcast(I32))
 
-        def load_wt(b):
-            for s in range(PASSES):
-                rows = wt[512 * s:512 * (s + 1), P * b:P * (b + 1)]
-                nc.sync.dma_start(out=wraw[b][:, s, :].rearrange("p (j c) -> p j c", j=4),
-                                  in_=rows.rearrange("(p j) c -> p j c", j=4))
+        def load_wt(h, s):
+            rows = wt[512 * s:512 * (s + 1), 256 * h:256 * (h + 1)]
+            nc.sync.dma_start(out=wraw[h, s][:], in_=rows.rearrange("(p j) c -> p j c", j=4))
 
         nc.sync.dma_start(offs_sb[:], offs)
-        nc.sync.dma_start(pos1_sb[:], pos1)
-        nc.sync.dma_start(pos2_sb[:], pos2)
-        nc.sync.dma_start(out=late_area[0:E, 0:P], in_=gate[0:1, :].rearrange("o (e u) -> (o e) u", u=C))
         for s in range(PASSES):
             nc.sync.dma_start(out=dyw[s], in_=dy_words[s].rearrange("p t d -> p (t d)").bitcast(I32))
         load_scales(dys, dy_scales.rearrange("s (q r) t -> r q s t", r=4))
+        nc.sync.dma_start(out=gate_rows[0:E, :], in_=gate[0:1, :].rearrange("o (e u) -> (o e) u", u=C))
         load_wb(0)
         load_scales(wbs[0], wbt_scales[0:2].rearrange("e s (q r) c -> r q (e s) c", r=4))
         load_wb(1)
         load_scales(wbs[1], wbt_scales[2:E].rearrange("e s (q r) c -> r q (e s) c", r=4))
         load_wb(2)
         load_wb(3)
-        load_wt(0)
-        load_wt(1)
+        load_wt(0, 0)
+        load_wt(0, 1)
+        nc.sync.dma_start(pos1_sb[:], pos1)
+        nc.sync.dma_start(pos2_sb[:], pos2)
         load_scales(was, wat_scales.rearrange("e s (q r) c -> r q (e s) c", r=4))
         load_wa(0)
-        load_wt(2)
+        load_wt(1, 0)
         load_wa(1)
-        load_wt(3)
+        load_wt(1, 1)
 
-        gbank = bank(3, "gbank")
+        gbank = bank(7, "gbank")
         nc.tensor.transpose(gbank[:, 0:P], gate_rows, ident[:])
         nc.scalar.activation(out=gcol[:], in_=gbank[:, 0:E], func=COPY)
 
@@ -164,11 +171,10 @@ def tile_moe_adb_none_kernel(
                         rhs_scale=(wbs[0][:, 2 * e + s, :] if e < 2 else wbs[1][:, 2 * (e - 2) + s, :]),
                         start=(s == 0), stop=(s == PASSES - 1))
                 dht = sb([P, H], BF16, "dht%d" % e)
-                for u0, u1 in (((0, 1), (1, 2)) if e == E - 1 else ((0, 2),)):
-                    nc.scalar.activation(
-                        out=dht[:].rearrange("c (u p h) -> c u p h", u=2, h=2)[:, u0:u1],
-                        in_=hbank[:].rearrange("c (p u h) -> c u p h", u=2, h=2)[:, u0:u1],
-                        func=COPY, scale=gcol[:, e:e + 1])
+                nc.scalar.activation(
+                    out=dht[:].rearrange("c (u p h) -> c u p h", u=2, h=2),
+                    in_=hbank[:].rearrange("c (p u h) -> c u p h", u=2, h=2),
+                    func=COPY, scale=gcol[:, e:e + 1])
                 pairs = dht[:].bitcast(F32)
                 for u in range(2):
                     at = P * (2 * (e - e0) + u)
@@ -184,20 +190,9 @@ def tile_moe_adb_none_kernel(
                 hc[e] = codes[:, C * (e - e0):C * (e - e0 + 1)]
                 hs[e] = scales[:, C * (e - e0):C * (e - e0 + 1)]
 
-        wc = [sb([P, PASSES, P], U32, "wc%d" % b) for b in range(BLOCKS)]
-        ws = [sb([P, PASSES, P], U8, "ws%d" % b) for b in range(BLOCKS)]
-        wt16 = [sb([P, PASSES * 512], BF16, "wt16%d" % b) for b in range(BLOCKS)]
-
-        def quantise_wt(b, copy):
-            copy(out=wt16[b][:].rearrange("p (s c i j) -> p s c j i", s=PASSES, i=4, j=4),
-                 in_=wraw[b][:].rearrange("p s (j c i) -> p s c j i", j=4, i=4))
-            nc.vector.quantize_mx(out=wc[b][:].rearrange("p s c -> p (s c)").bitcast(FP8X4),
-                                  scales=ws[b][:].rearrange("p s c -> p (s c)"), in_=wt16[b][:])
-
         dx = [sb([P, S], F32, "dx%d" % b) for b in range(BLOCKS)]
-        base = [sb([P, T], F32, "base%d" % b) for b in range(BLOCKS)]
 
-        def adapters(b, e0, e1, number):
+        def adapters(b, e0, e1, number, copy):
             dbank = bank(number, "dbank%d%d" % (b, e0))
             for e in range(e0, e1):
                 at = 512 * e + 2 * P * (b % 2)
@@ -206,102 +201,131 @@ def tile_moe_adb_none_kernel(
                     lhsT=wa_words[b // 2][:, at:at + 2 * P].bitcast(FP4X4),
                     lhsT_scale=was[:, e, P * b:P * (b + 1)],
                     rhs=hc[e].bitcast(FP8X4), rhs_scale=hs[e], start=True, stop=True)
-            nc.scalar.copy(out=dx[b][:, C * e0:C * e1], in_=dbank[:, 0:C * (e1 - e0)])
+            copy(out=dx[b][:, C * e0:C * e1], in_=dbank[:, 0:C * (e1 - e0)])
+
+        wc = {}
+        ws = {}
+
+        def round_wt(h, s, copy, at):
+            wt16 = place([P, 1024], BF16, "wt16%d%d" % (h, s), at)
+            copy(out=wt16[:].rearrange("p (c i j) -> p c j i", i=4, j=4),
+                 in_=wraw[h, s][:].rearrange("p j (c i) -> p c j i", i=4))
+            wc[h, s] = sb([P, 256], U32, "wc%d%d" % (h, s))
+            ws[h, s] = sb([P, 256], U8, "ws%d%d" % (h, s))
+            nc.vector.quantize_mx(out=wc[h, s][:].bitcast(FP8X4), scales=ws[h, s][:], in_=wt16[:])
+
+        base = {}
 
         def frozen(b, number):
-            bbank = bank(number, "bbank%d" % b)
+            base[b] = bank(number, "base%d" % b)
+            cols = slice(P * (b % 2), P * (b % 2 + 1))
             for s in range(PASSES):
                 nc.tensor.matmul_mx(
-                    out=bbank[:], lhsT=wc[b][:, s, :].bitcast(FP8X4), lhsT_scale=ws[b][:, s, :],
+                    out=base[b][:], lhsT=wc[b // 2, s][:, cols].bitcast(FP8X4), lhsT_scale=ws[b // 2, s][:, cols],
                     rhs=dyw[s].bitcast(FP8X4), rhs_scale=dys[:, s, :], start=(s == 0), stop=(s == PASSES - 1))
-            nc.scalar.copy(out=base[b][:], in_=bbank[:])
 
         ys = sb([P, BLOCKS, P], U8, "ys")
         yt = [sb([P, K], BF16, "yt%d" % b) for b in range(BLOCKS)]
         yb = [sb([P, 4 * P], BF16, "yb%d" % b) for b in range(BLOCKS)]
-        part = {}
-        y = {}
-        last = BLOCKS - 1
+        y = [sb([P, T], F32, "y%d" % b) for b in range(BLOCKS)]
+        second = {}
+        both = {}
 
-        def first_slot(b, x0, x1):
-            if (b, x0) == (last, last):
-                under_codes = place([P, T], F32, "part33", CODES_AT)
-                part[b, x0] = under_codes[:, 0:P]
-            else:
-                part[b, x0] = sb([P, P * (x1 - x0)], F32, "part%d%d" % (b, x0))[:]
-            nc.vector.tensor_tensor(part[b, x0], dx[b][:].indirect(pos1_sb[:, 8 * x0:8 * x1]),
-                                    base[b][:, P * x0:P * x1], ADD)
+        def gather_second(b):
+            for h in range(2):
+                at = SECOND_AT + 2048 * (2 * b + h)
+                second[b, h] = place([P, 256], F32, "second%d%d" % (b, h), at)
+                nc.scalar.activation(out=second[b, h][:], in_=dx[b][:].indirect(pos2_sb[:, 16 * h:16 * (h + 1)]),
+                                     func=COPY)
 
-        def second_slot(b, x0, x1):
-            nc.vector.tensor_tensor(y[b][:, P * x0:P * x1], dx[b][:].indirect(pos2_sb[:, 8 * x0:8 * x1]),
-                                    part[b, x0], ADD)
+        def gather_first(b, h):
+            both[b, h] = place([P, 256], F32, "both%d%d" % (b, h), BOTH_AT + 1024 * ((2 * b + h) % 3))
+            nc.vector.tensor_tensor(both[b, h][:], dx[b][:].indirect(pos1_sb[:, 16 * h:16 * (h + 1)]),
+                                    second[b, h][:], ADD)
 
-        def turn(b, x0, x1, number):
+        def add_base(b, x0, x1):
+            cols = slice(P * x0, P * x1)
+            nc.vector.tensor_tensor(y[b][:, cols], both[b, x0 // 2][:, P * (x0 % 2):P * (x0 % 2 + x1 - x0)],
+                                    base[b][:, cols], ADD)
+
+        def turn(b, x0, x1, number, copy):
             if x1 == 4:
                 nc.sync.dma_start(out=out_0[P * b:P * (b + 1), :], in_=y[b][:])
             tbank = bank(number, "tbank%d%d" % (b, x0))
             for x in range(x0, x1):
                 nc.tensor.transpose(tbank[:, P * (x - x0):P * (x - x0 + 1)], y[b][:, P * x:P * (x + 1)], ident[:])
-            nc.scalar.copy(
+            copy(
                 out=yt[b][:].rearrange("c (u p h) -> c u p h", u=2, h=2)[:, :, 32 * x0:32 * x1, :],
                 in_=tbank[:, 0:P * (x1 - x0)].rearrange("c (p u h) -> c u p h", u=2, h=2))
 
-        def combine(b, number):
-            y[b] = sb([P, T], F32, "y%d" % b)
-            for x0 in (0, 2):
-                first_slot(b, x0, x0 + 2)
-            for x0 in (0, 2):
-                second_slot(b, x0, x0 + 2)
-            turn(b, 0, 4, number)
+        word_rows = out_1[0].rearrange("p t d -> p (t d)").bitcast(I32)
 
-        def weave(b, number):
+        def planes(b, number, copy):
             xbank = bank(number, "xbank%d" % b)
             pairs = yt[b][:].bitcast(F32)
             for u in range(2):
                 nc.tensor.transpose(xbank[:, P * u:P * (u + 1)], pairs[:, P * u:P * (u + 1)], ident[:])
-            nc.scalar.copy(out=yb[b][:].bitcast(F32).rearrange("p (c u) -> p c u", u=2),
-                           in_=xbank[:, 0:2 * P].rearrange("p (u c) -> p c u", u=2))
+            copy(out=yb[b][:].bitcast(F32).rearrange("p (c u) -> p c u", u=2),
+                 in_=xbank[:, 0:2 * P].rearrange("p (u c) -> p c u", u=2))
+            if b in (1, 2):
+                yc = place([P, P], U32, "yc%d" % b, SECOND_AT + 2048 * 7 + 512 * (b - 1))
+            else:
+                yc = sb([P, P], U32, "yc%d" % b)
+            nc.vector.quantize_mx(out=yc[:].bitcast(FP8X4), scales=ys[:, b, :], in_=yb[b][:])
+            nc.sync.dma_start(out=word_rows[32 * b:32 * (b + 1), :].rearrange("q (x t) -> x q t", x=4),
+                              in_=yc[:].bitcast(I32))
 
-        quantise_wt(0, nc.vector.tensor_copy)
-        quantise_wt(1, nc.vector.tensor_copy)
-        adapters(0, 0, 4, 0)
-        frozen(0, 1)
-        adapters(0, 4, 7, 5)
-        adapters(0, 7, 8, 6)
-        quantise_wt(2, nc.vector.tensor_copy)
-        adapters(1, 0, 4, 1)
-        adapters(1, 4, 8, 5)
-        frozen(1, 6)
-        quantise_wt(3, nc.scalar.copy)
-        adapters(2, 0, 4, 0)
-        adapters(2, 4, 8, 1)
-        frozen(2, 5)
-        combine(0, 6)
-        adapters(3, 0, 4, 0)
-        adapters(3, 4, 8, 1)
-        weave(0, 5)
-        frozen(3, 6)
-        combine(1, 0)
-        combine(2, 1)
-        weave(1, 5)
-        weave(2, 6)
-        y[last] = sb([P, T], F32, "y3")
-        first_slot(last, 0, 2)
-        first_slot(last, 2, 3)
-        second_slot(last, 0, 2)
-        first_slot(last, 3, 4)
-        second_slot(last, 2, 3)
-        turn(last, 0, 3, 1)
-        second_slot(last, 3, 4)
-        turn(last, 3, 4, 5)
-        weave(last, 0)
+        on_vector = nc.vector.tensor_copy
+        on_scalar = nc.scalar.copy
 
-        yc = place([P, BLOCKS, P], U32, "yc", CODES_AT)
-        for b in range(BLOCKS):
-            nc.vector.quantize_mx(out=yc[:, b, :].bitcast(FP8X4), scales=ys[:, b, :], in_=yb[b][:])
-        word_rows = out_1[0].rearrange("p t d -> p (t d)").bitcast(I32).rearrange("(b q) t -> q b t", b=BLOCKS)
+        round_wt(0, 0, on_vector, WT16_AT)
+        round_wt(0, 1, on_vector, WT16_AT + 2048)
+        adapters(0, 0, 4, 5, on_scalar)
+        adapters(0, 4, 7, 7, on_scalar)
+        adapters(0, 7, 8, 2, on_scalar)
+        round_wt(1, 0, on_vector, WT16_AT + 4096)
+        gather_second(0)
+        adapters(1, 0, 4, 2, on_scalar)
+        adapters(1, 4, 8, 0, on_scalar)
+        frozen(0, 5)
+        gather_first(0, 0)
+        gather_first(0, 1)
+        frozen(1, 7)
+        gather_second(1)
+        adapters(2, 0, 4, 2, on_scalar)
+        adapters(2, 4, 8, 1, on_scalar)
+        add_base(0, 0, 2)
+        gather_first(1, 0)
+        add_base(0, 2, 4)
+        turn(0, 0, 4, 3, on_scalar)
+        gather_first(1, 1)
+        round_wt(1, 1, on_vector, SECOND_AT + 2 * 2048)
+        gather_second(2)
+        add_base(1, 0, 2)
+        add_base(1, 2, 4)
+        frozen(2, 6)
+        frozen(3, 0)
+        adapters(3, 0, 4, 2, on_scalar)
+        adapters(3, 4, 8, 1, on_scalar)
+        gather_second(3)
+        turn(1, 0, 4, 4, on_scalar)
+        gather_first(2, 0)
+        gather_first(2, 1)
+        planes(0, 5, on_scalar)
+        add_base(2, 0, 2)
+        gather_first(3, 0)
+        add_base(2, 2, 4)
+        turn(2, 0, 4, 3, on_scalar)
+        gather_first(3, 1)
+        planes(1, 7, on_scalar)
+        add_base(3, 0, 2)
+        add_base(3, 2, 4)
+        turn(3, 0, 2, 4, on_vector)
+        turn(3, 2, 4, 1, on_vector)
+        planes(2, 2, on_scalar)
+        planes(3, 5, on_vector)
+
         scale_rows = out_2[0].rearrange("(b g) t -> g b t", g=4)
         for x in range(4):
-            nc.sync.dma_start(out=word_rows[:, :, P * x:P * (x + 1)], in_=yc[32 * x:32 * (x + 1)].bitcast(I32))
             nc.scalar.dma_start(out=scale_rows[:, :, P * x:P * (x + 1)].bitcast(I32),
                                 in_=ys[32 * x:32 * x + 4].bitcast(I32))

@@ -258,8 +258,6 @@ def tile_moe_adb_none_kernel(
                 out=yt[b][:].rearrange("c (u p h) -> c u p h", u=2, h=2)[:, :, 32 * x0:32 * x1, :],
                 in_=tbank[:, 0:P * (x1 - x0)].rearrange("c (p u h) -> c u p h", u=2, h=2))
 
-        word_rows = out_1[0].rearrange("p t d -> p (t d)").bitcast(I32)
-
         def planes(b, number, copy):
             xbank = bank(number, "xbank%d" % b)
             pairs = yt[b][:].bitcast(F32)
@@ -267,13 +265,6 @@ def tile_moe_adb_none_kernel(
                 nc.tensor.transpose(xbank[:, P * u:P * (u + 1)], pairs[:, P * u:P * (u + 1)], ident[:])
             copy(out=yb[b][:].bitcast(F32).rearrange("p (c u) -> p c u", u=2),
                  in_=xbank[:, 0:2 * P].rearrange("p (u c) -> p c u", u=2))
-            if b in (1, 2):
-                yc = place([P, P], U32, "yc%d" % b, SECOND_AT + 2048 * 7 + 512 * (b - 1))
-            else:
-                yc = sb([P, P], U32, "yc%d" % b)
-            nc.vector.quantize_mx(out=yc[:].bitcast(FP8X4), scales=ys[:, b, :], in_=yb[b][:])
-            nc.sync.dma_start(out=word_rows[32 * b:32 * (b + 1), :].rearrange("q (x t) -> x q t", x=4),
-                              in_=yc[:].bitcast(I32))
 
         on_vector = nc.vector.tensor_copy
         on_scalar = nc.scalar.copy
@@ -325,7 +316,12 @@ def tile_moe_adb_none_kernel(
         planes(2, 2, on_scalar)
         planes(3, 5, on_vector)
 
+        yc = place([P, BLOCKS, P], U32, "yc", SECOND_AT + 2048 * 7)
+        for b in range(BLOCKS):
+            nc.vector.quantize_mx(out=yc[:, b, :].bitcast(FP8X4), scales=ys[:, b, :], in_=yb[b][:])
+        word_rows = out_1[0].rearrange("p t d -> p (t d)").bitcast(I32).rearrange("(b q) t -> q b t", b=BLOCKS)
         scale_rows = out_2[0].rearrange("(b g) t -> g b t", g=4)
         for x in range(4):
+            nc.sync.dma_start(out=word_rows[:, :, P * x:P * (x + 1)], in_=yc[32 * x:32 * (x + 1)].bitcast(I32))
             nc.scalar.dma_start(out=scale_rows[:, :, P * x:P * (x + 1)].bitcast(I32),
                                 in_=ys[32 * x:32 * x + 4].bitcast(I32))

@@ -21,11 +21,11 @@ FP4X4 = mybir.dt.float4_e2m1fn_x4
 COPY = mybir.ActivationFunctionType.Copy
 ADD = mybir.AluOpType.add
 
-FIRST_AREA = 0
+FIRST_AREA = 110592
 SECOND_AREA = 12288
 LATE_AREA = 32768
 PLANE_AT = 512
-WB_WORDS_AT = (4096, 8192, 24576, 28672)
+WB_WORDS_AT = (FIRST_AREA + 4608, FIRST_AREA + 8704, FIRST_AREA + 12800, 28672)
 WA_WORDS_AT = 40960
 WT_AT = (49152, 53248, 57344, 61440)
 SECOND_AT = 65536
@@ -63,7 +63,7 @@ def tile_moe_adb_none_kernel(
         ident = sb([P, P], F32, "ident")
         gcol = sb([P, E], F32, "gcol")
         gate_rows = place([P, 1920], F32, "gate_area", GATHERED_AT)[:, 0:P]
-        first_area = place([P, 3072], F32, "first_area", FIRST_AREA)
+        first_area = place([P, 4224], F32, "first_area", FIRST_AREA)
         second_area = place([P, 5120], F32, "second_area", SECOND_AREA)
         late_area = place([P, 8192], F32, "late_area", LATE_AREA)
 
@@ -81,15 +81,14 @@ def tile_moe_adb_none_kernel(
         nc.gpsimd.memset(gate_rows, 0.0)
         zeros = sb([P, P], F32, "zeros")
         nc.gpsimd.memset(zeros[:], 0.0)
-        clear_on_vector(first_area, plane, 512)
-        clear_on_vector(second_area, plane, 512)
+        clear_on_vector(first_area, plane, 1024)
         nc.gpsimd.affine_select(out=ident[:], in_=zeros[:], compare_op=mybir.AluOpType.not_equal, fill=1.0,
                                 base=0, pattern=[[-1, P]], channel_multiplier=1)
-        nc.gpsimd.memset(second_area[:, plane + 512:plane + 1024].bitcast(I32), 0)
-        clear_on_scalar(second_area, plane + 1024, 512)
+        nc.gpsimd.memset(second_area[:, plane:plane + 512].bitcast(I32), 0)
+        clear_on_scalar(second_area, plane + 512, 512)
         clear_on_scalar(late_area, plane, 1024)
-        wbs = [place([P, 2 * PASSES, H], U8, "wbs0", FIRST_AREA + PLANE_AT),
-               place([P, (E - 2) * PASSES, H], U8, "wbs1", SECOND_AREA + PLANE_AT)]
+        wbs = [place([P, 4 * PASSES, H], U8, "wbs0", FIRST_AREA + PLANE_AT),
+               place([P, 4 * PASSES, H], U8, "wbs1", SECOND_AREA + PLANE_AT)]
         was = place([P, E, K], U8, "was", LATE_AREA + PLANE_AT)
         wb_words = [place([P, 4096], U8, "wbw%d" % j, WB_WORDS_AT[j]) for j in range(PAIRS)]
         wa_words = [place([P, 4096], U8, "waw%d" % h, WA_WORDS_AT + 4096 * h) for h in range(2)]
@@ -120,10 +119,10 @@ def tile_moe_adb_none_kernel(
         load_scales(dys, dy_scales.rearrange("s (q r) t -> r q s t", r=4))
         nc.sync.dma_start(out=gate_rows[0:E, :], in_=gate[0:1, :].rearrange("o (e u) -> (o e) u", u=C))
         load_wb(0)
-        load_scales(wbs[0], wbt_scales[0:2].rearrange("e s (q r) c -> r q (e s) c", r=4))
+        load_scales(wbs[0], wbt_scales[0:4].rearrange("e s (q r) c -> r q (e s) c", r=4))
         load_wb(1)
-        load_scales(wbs[1], wbt_scales[2:E].rearrange("e s (q r) c -> r q (e s) c", r=4))
         load_wb(2)
+        load_scales(wbs[1], wbt_scales[4:E].rearrange("e s (q r) c -> r q (e s) c", r=4))
         load_wb(3)
         load_wt(0, 0)
         load_wt(0, 1)
@@ -168,7 +167,7 @@ def tile_moe_adb_none_kernel(
                     nc.tensor.matmul_mx(
                         out=hbank[:], lhsT=gw[e0, s][:, slots].bitcast(FP8X4), lhsT_scale=gs[e0, s][:, slots],
                         rhs=wb_words[e // 2][:, at:at + 1024].bitcast(FP4X4),
-                        rhs_scale=(wbs[0][:, 2 * e + s, :] if e < 2 else wbs[1][:, 2 * (e - 2) + s, :]),
+                        rhs_scale=wbs[e // 4][:, 2 * (e % 4) + s, :],
                         start=(s == 0), stop=(s == PASSES - 1))
                 dht = sb([P, H], BF16, "dht%d" % e)
                 nc.scalar.activation(

@@ -282,7 +282,7 @@ def tile_moe_adb_none_kernel(
         gather_first(0, 1)
         frozen(1, 7)
         gather_second(1)
-        adapters(2, 0, 4, 2, on_scalar)
+        adapters(2, 0, 4, 2, on_vector)
         adapters(2, 4, 8, 1, on_scalar)
         add_base(0, 0, 2)
         gather_first(1, 0)
@@ -310,7 +310,7 @@ def tile_moe_adb_none_kernel(
         planes(1, 7, on_scalar)
         add_base(3, 0, 2)
         add_base(3, 2, 4)
-        turn(3, 0, 2, 4, on_vector)
+        turn(3, 0, 2, 4, on_scalar)
         turn(3, 2, 4, 1, on_vector)
         planes(2, 2, on_scalar)
         planes(3, 5, on_vector)

@@ -77,14 +77,15 @@ def tile_moe_adb_none_kernel(
                            in_=zeros[:].bitcast(U32).unsqueeze(1).to_broadcast([P, words // P, P]))
 
         plane = PLANE_AT // 4
-        nc.gpsimd.memset(dys[:].bitcast(I32), 0)
-        nc.gpsimd.memset(gate_rows, 0.0)
+        nc.gpsimd.memset(ident[:], 0.0)
         zeros = sb([P, P], F32, "zeros")
-        nc.gpsimd.memset(zeros[:], 0.0)
+        clear_on_vector(dys[:].rearrange("p s t -> p (s t)").bitcast(F32), 0, 256)
+        clear_on_vector(gate_rows, 0, P)
+        clear_on_vector(zeros, 0, P)
         clear_on_vector(first_area, plane, 1024)
-        nc.gpsimd.affine_select(out=ident[:], in_=zeros[:], compare_op=mybir.AluOpType.not_equal, fill=1.0,
+        nc.gpsimd.affine_select(out=ident[:], in_=ident[:], compare_op=mybir.AluOpType.not_equal, fill=1.0,
                                 base=0, pattern=[[-1, P]], channel_multiplier=1)
-        nc.gpsimd.memset(second_area[:, plane:plane + 512].bitcast(I32), 0)
+        clear_on_vector(second_area, plane, 512)
         clear_on_scalar(second_area, plane + 512, 512)
         clear_on_scalar(late_area, plane, 1024)
         wbs = [place([P, 4 * PASSES, H], U8, "wbs0", FIRST_AREA + PLANE_AT),

@@ -33,6 +33,9 @@ GATHERED_AT = 90112
 WT16_AT = 98304
 BOTH_AT = 81920
 
+SUM_BANKS = (0, 1, 2, 5, 6, 0, 1, 2)
+TURN_BANKS = (4, 3, 4, 3, 6)
+WOVEN_BEHIND = {4: (0,), 6: (1,), 8: (2, 3, 4)}
 GROUPS = ((0, 2), (2, 4), (4, 6), (6, 7), (7, 8))
 
 
@@ -156,26 +159,14 @@ def tile_moe_adb_none_kernel(
                 nc.vector.tensor_copy(out=gs[e0, s][:], in_=dys[:, s, :].indirect(cut))
 
         hc = {}
+        dhts = {}
         hs = {}
-        for g, (e0, e1) in enumerate(GROUPS):
+        def weave_dh(g):
+            e0, e1 = GROUPS[g]
             n = C * (e1 - e0)
-            wbank = bank(4 - g % 2, "wbank%d" % e0)
+            wbank = bank(TURN_BANKS[g], "wbank%d" % e0)
             for e in range(e0, e1):
-                hbank = bank(e % 3, "hbank%d" % e)
-                slots = slice(C * (e - e0), C * (e - e0 + 1))
-                for s in range(PASSES):
-                    at = 1024 * (2 * (e % 2) + s)
-                    nc.tensor.matmul_mx(
-                        out=hbank[:], lhsT=gw[e0, s][:, slots].bitcast(FP8X4), lhsT_scale=gs[e0, s][:, slots],
-                        rhs=wb_words[e // 2][:, at:at + 1024].bitcast(FP4X4),
-                        rhs_scale=wbs[e // 4][:, 2 * (e % 4) + s, :],
-                        start=(s == 0), stop=(s == PASSES - 1))
-                dht = sb([P, H], BF16, "dht%d" % e)
-                nc.scalar.activation(
-                    out=dht[:].rearrange("c (u p h) -> c u p h", u=2, h=2),
-                    in_=hbank[:].rearrange("c (p u h) -> c u p h", u=2, h=2),
-                    func=COPY, scale=gcol[:, e:e + 1])
-                pairs = dht[:].bitcast(F32)
+                pairs = dhts[e][:].bitcast(F32)
                 for u in range(2):
                     at = P * (2 * (e - e0) + u)
                     nc.tensor.transpose(wbank[:, at:at + P], pairs[:, P * u:P * (u + 1)], ident[:])
@@ -189,6 +180,26 @@ def tile_moe_adb_none_kernel(
             for e in range(e0, e1):
                 hc[e] = codes[:, C * (e - e0):C * (e - e0 + 1)]
                 hs[e] = scales[:, C * (e - e0):C * (e - e0 + 1)]
+
+        for e0, e1 in GROUPS:
+            for e in range(e0, e1):
+                hbank = bank(SUM_BANKS[e], "hbank%d" % e)
+                slots = slice(C * (e - e0), C * (e - e0 + 1))
+                for s in range(PASSES):
+                    at = 1024 * (2 * (e % 2) + s)
+                    nc.tensor.matmul_mx(
+                        out=hbank[:], lhsT=gw[e0, s][:, slots].bitcast(FP8X4), lhsT_scale=gs[e0, s][:, slots],
+                        rhs=wb_words[e // 2][:, at:at + 1024].bitcast(FP4X4),
+                        rhs_scale=wbs[e // 4][:, 2 * (e % 4) + s, :],
+                        start=(s == 0), stop=(s == PASSES - 1))
+                dht = sb([P, H], BF16, "dht%d" % e)
+                nc.scalar.activation(
+                    out=dht[:].rearrange("c (u p h) -> c u p h", u=2, h=2),
+                    in_=hbank[:].rearrange("c (p u h) -> c u p h", u=2, h=2),
+                    func=COPY, scale=gcol[:, e:e + 1])
+                dhts[e] = dht
+            for late in WOVEN_BEHIND.get(e1, ()):
+                weave_dh(late)
 
         dx = [sb([P, S], F32, "dx%d" % b) for b in range(BLOCKS)]
 

@@ -171,7 +171,8 @@ def tile_moe_adb_none_kernel(
                     at = P * (2 * (e - e0) + u)
                     nc.tensor.transpose(wbank[:, at:at + P], pairs[:, P * u:P * (u + 1)], ident[:])
             dhb = sb([P, 4 * n], BF16, "dhb%d" % e0)
-            nc.scalar.copy(
+            weaver = nc.vector.tensor_copy if g == 2 else nc.scalar.copy
+            weaver(
                 out=dhb[:].bitcast(F32).rearrange("p (x c u) -> p x c u", c=C, u=2),
                 in_=wbank[:, 0:2 * n].rearrange("p (x u c) -> p x c u", c=C, u=2))
             codes = sb([P, n], U32, "hc%d" % e0)

@@ -66,7 +66,7 @@ def tile_moe_adb_none_kernel(
         ident = sb([P, P], F32, "ident")
         gcol = sb([P, E], F32, "gcol")
         gate_rows = place([P, 1920], F32, "gate_area", GATHERED_AT)[:, 0:P]
-        first_area = place([P, 4224], F32, "first_area", FIRST_AREA)
+        first_area = place([P, 1152], F32, "first_area", FIRST_AREA)
         second_area = place([P, 5120], F32, "second_area", SECOND_AREA)
         late_area = place([P, 8192], F32, "late_area", LATE_AREA)
 
@@ -82,10 +82,10 @@ def tile_moe_adb_none_kernel(
         plane = PLANE_AT // 4
         nc.gpsimd.memset(ident[:], 0.0)
         zeros = sb([P, P], F32, "zeros")
-        clear_on_vector(dys[:].rearrange("p s t -> p (s t)").bitcast(F32), 0, 256)
-        clear_on_vector(gate_rows, 0, P)
-        clear_on_vector(zeros, 0, P)
-        clear_on_vector(first_area, plane, 1024)
+        nc.vector.memset(dys[:].rearrange("p s t -> p (s t)").bitcast(I32), 0)
+        nc.vector.memset(first_area[:, plane:plane + 1024].bitcast(I32), 0)
+        nc.vector.memset(gate_rows.bitcast(I32), 0)
+        nc.vector.memset(zeros[:].bitcast(I32), 0)
         nc.gpsimd.affine_select(out=ident[:], in_=ident[:], compare_op=mybir.AluOpType.not_equal, fill=1.0,
                                 base=0, pattern=[[-1, P]], channel_multiplier=1)
         clear_on_vector(second_area, plane, 512)

@@ -29,7 +29,7 @@ WB_WORDS_AT = (FIRST_AREA + 4608, FIRST_AREA + 8704, FIRST_AREA + 12800, 28672)
 WA_WORDS_AT = 40960
 WT_AT = (49152, 53248, 57344, 61440)
 SECOND_AT = 65536
-GATHERED_AT = 90112
+GATHERED_AT = 88064
 WT16_AT = 98304
 BOTH_AT = 81920
 
@@ -50,10 +50,10 @@ def tile_moe_adb_none_kernel(
         psum = ctx.enter_context(tc.psum_pool(name="psum", bufs=1))
 
         def sb(shape, dtype, name):
-            return keep.tile(shape, dtype, name=name, align_bytes=64)
+            return keep.tile(shape, dtype, name=name, align_bytes=256)
 
         def place(shape, dtype, name, offset):
-            return laid.tile(shape, dtype, name=name, align_bytes=64, offset=offset)
+            return laid.tile(shape, dtype, name=name, align_bytes=256, offset=offset)
 
         def bank(number, name):
             return psum.tile([P, 512], F32, name=name, offset=2048 * number)
@@ -65,7 +65,7 @@ def tile_moe_adb_none_kernel(
         dys = sb([P, PASSES, T], U8, "dys")
         ident = sb([P, P], F32, "ident")
         gcol = sb([P, E], F32, "gcol")
-        gate_rows = place([P, 1920], F32, "gate_area", GATHERED_AT)[:, 0:P]
+        gate_rows = place([P, 2304], F32, "gate_area", GATHERED_AT)[:, 0:P]
         first_area = place([P, 1152], F32, "first_area", FIRST_AREA)
         second_area = place([P, 5120], F32, "second_area", SECOND_AREA)
         late_area = place([P, 8192], F32, "late_area", LATE_AREA)
@@ -152,7 +152,7 @@ def tile_moe_adb_none_kernel(
                     gw[e0, s] = sb([P, n], U32, "gw%d%d" % (e0, s))
                     gs[e0, s] = sb([P, n], U8, "gs%d%d" % (e0, s))
                 else:
-                    at = GATHERED_AT + 5 * (C * PASSES * (e0 - 2) + n * s)
+                    at = GATHERED_AT + 768 * (PASSES * (e0 - 2) + (e1 - e0) * s)
                     gw[e0, s] = place([P, n], U32, "gw%d%d" % (e0, s), at)
                     gs[e0, s] = place([P, n], U8, "gs%d%d" % (e0, s), at + 4 * n)
                 nc.vector.tensor_copy(out=gw[e0, s][:], in_=dyw[s].bitcast(U32).indirect(cut))
@@ -333,7 +333,7 @@ def tile_moe_adb_none_kernel(
             nc.vector.quantize_mx(out=yc[:, b, :].bitcast(FP8X4), scales=ys[:, b, :], in_=yb[b][:])
         word_rows = out_1[0].rearrange("p t d -> p (t d)").bitcast(I32).rearrange("(b q) t -> q b t", b=BLOCKS)
         scale_rows = out_2[0].rearrange("(b g) t -> g b t", g=4)
-        for x in range(4):
+        for x in (0, 2, 1, 3):
             nc.sync.dma_start(out=word_rows[:, :, P * x:P * (x + 1)], in_=yc[32 * x:32 * (x + 1)].bitcast(I32))
             nc.scalar.dma_start(out=scale_rows[:, :, P * x:P * (x + 1)].bitcast(I32),
                                 in_=ys[32 * x:32 * x + 4].bitcast(I32))

from contextlib import ExitStack

import concourse.mybir as mybir

K, T, E, C, H, N = 512, 512, 8, 128, 512, 1024
S = E * C
P = 128
PASSES = N // 512
PAIRS = E // 2
BLOCKS = K // P
FLOPS = 2 * N * K * T + 2 * N * H * S + 2 * H * K * S

F32 = mybir.dt.float32
BF16 = mybir.dt.bfloat16
I32 = mybir.dt.int32
U32 = mybir.dt.uint32
U16 = mybir.dt.uint16
U8 = mybir.dt.uint8
FP8X4 = mybir.dt.float8_e4m3fn_x4
FP4X4 = mybir.dt.float4_e2m1fn_x4
COPY = mybir.ActivationFunctionType.Copy
ADD = mybir.AluOpType.add

FIRST_AREA = 110592
SECOND_AREA = 12288
LATE_AREA = 32768
PLANE_AT = 512
WB_WORDS_AT = (FIRST_AREA + 4608, FIRST_AREA + 8704, FIRST_AREA + 12800, 28672)
WA_WORDS_AT = 40960
WT_AT = (49152, 53248, 57344, 61440)
SECOND_AT = 65536
GATHERED_AT = 88064
WT16_AT = 98304
BOTH_AT = 81920

SUM_BANKS = (0, 1, 2, 5, 6, 0, 1, 2)
TURN_BANKS = (4, 3, 4, 3, 6)
WOVEN_BEHIND = {4: (0,), 6: (1,), 8: (2, 3, 4)}
GROUPS = ((0, 2), (2, 4), (4, 6), (6, 7), (7, 8))


def tile_moe_adb_none_kernel(
    tc, dy_words, dy_scales, wt, wbt_words, wbt_scales, wat_words, wat_scales, gate, offs, pos1, pos2,
    out_0, out_1, out_2,
):
    nc = tc.nc
    with ExitStack() as ctx:
        keep = ctx.enter_context(tc.tile_pool(name="keep", bufs=1))
        laid = ctx.enter_context(tc.tile_pool(name="laid", bufs=1))
        psum = ctx.enter_context(tc.psum_pool(name="psum", bufs=1))

        def sb(shape, dtype, name):
            return keep.tile(shape, dtype, name=name, align_bytes=256)

        def place(shape, dtype, name, offset):
            return laid.tile(shape, dtype, name=name, align_bytes=256, offset=offset)

        def bank(number, name):
            return psum.tile([P, 512], F32, name=name, offset=2048 * number)

        offs_sb = keep.tile([P, S // 16], U16, name="offs_sb")
        pos1_sb = keep.tile([P, T // 16], U16, name="pos1_sb")
        pos2_sb = keep.tile([P, T // 16], U16, name="pos2_sb")
        dyw = [sb([P, T], I32, "dyw%d" % s)[:] for s in range(PASSES)]
        dys = sb([P, PASSES, T], U8, "dys")
        ident = sb([P, P], F32, "ident")
        gcol = sb([P, E], F32, "gcol")
        gate_rows = place([P, 2304], F32, "gate_area", GATHERED_AT)[:, 0:P]
        first_area = place([P, 1152], F32, "first_area", FIRST_AREA)
        second_area = place([P, 5120], F32, "second_area", SECOND_AREA)
        late_area = place([P, 8192], F32, "late_area", LATE_AREA)

        def clear_on_vector(area, start, words):
            cut = words // 2 - 1
            for w0, w1 in ((0, cut), (cut, words)):
                nc.vector.memset(area[:, start + w0:start + w1].bitcast(I32), 0)

        def clear_on_scalar(area, start, words):
            nc.scalar.copy(out=area[:, start:start + words].bitcast(U32).rearrange("p (a c) -> p a c", c=P),
                           in_=zeros[:].bitcast(U32).unsqueeze(1).to_broadcast([P, words // P, P]))

        plane = PLANE_AT // 4
        nc.gpsimd.memset(ident[:], 0.0)
        zeros = sb([P, P], F32, "zeros")
        nc.vector.memset(dys[:].rearrange("p s t -> p (s t)").bitcast(I32), 0)
        nc.vector.memset(first_area[:, plane:plane + 1024].bitcast(I32), 0)
        nc.vector.memset(gate_rows.bitcast(I32), 0)
        nc.vector.memset(zeros[:].bitcast(I32), 0)
        nc.gpsimd.affine_select(out=ident[:], in_=ident[:], compare_op=mybir.AluOpType.not_equal, fill=1.0,
                                base=0, pattern=[[-1, P]], channel_multiplier=1)
        clear_on_vector(second_area, plane, 512)
        clear_on_scalar(second_area, plane + 512, 512)
        clear_on_scalar(late_area, plane, 1024)
        wbs = [place([P, 4 * PASSES, H], U8, "wbs0", FIRST_AREA + PLANE_AT),
               place([P, 4 * PASSES, H], U8, "wbs1", SECOND_AREA + PLANE_AT)]
        was = place([P, E, K], U8, "was", LATE_AREA + PLANE_AT)
        wb_words = [place([P, 4096], U8, "wbw%d" % j, WB_WORDS_AT[j]) for j in range(PAIRS)]
        wa_words = [place([P, 4096], U8, "waw%d" % h, WA_WORDS_AT + 4096 * h) for h in range(2)]
        wraw = {}
        for h in range(2):
            for s in range(PASSES):
                wraw[h, s] = place([P, 4, 256], F32, "wraw%d%d" % (h, s), WT_AT[2 * h + s])

        def load_scales(plane, rows):
            for r in range(4):
                nc.sync.dma_start(out=plane[r:P:32].bitcast(I32), in_=rows[r].bitcast(I32))

        def load_wb(j):
            nc.sync.dma_start(out=wb_words[j][:].bitcast(I32).rearrange("p (x c) -> p x c", x=4),
                              in_=wbt_words[2 * j:2 * j + 2].rearrange("e s p c -> p (e s) c").bitcast(I32))

        def load_wa(h):
            nc.sync.dma_start(out=wa_words[h][:].bitcast(I32).rearrange("p (e c) -> p e c", e=E),
                              in_=wat_words[:, 0, :, 512 * h:512 * (h + 1)].rearrange("e p c -> p e c").bitcast(I32))

        def load_wt(h, s):
            rows = wt[512 * s:512 * (s + 1), 256 * h:256 * (h + 1)]
            nc.sync.dma_start(out=wraw[h, s][:], in_=rows.rearrange("(p j) c -> p j c", j=4))

        nc.sync.dma_start(offs_sb[:], offs)
        for s in range(PASSES):
            nc.sync.dma_start(out=dyw[s], in_=dy_words[s].rearrange("p t d -> p (t d)").bitcast(I32))
        load_scales(dys, dy_scales.rearrange("s (q r) t -> r q s t", r=4))
        nc.sync.dma_start(out=gate_rows[0:E, :], in_=gate[0:1, :].rearrange("o (e u) -> (o e) u", u=C))
        load_wb(0)
        load_scales(wbs[0], wbt_scales[0:4].rearrange("e s (q r) c -> r q (e s) c", r=4))
        load_wb(1)
        load_wb(2)
        load_scales(wbs[1], wbt_scales[4:E].rearrange("e s (q r) c -> r q (e s) c", r=4))
        load_wb(3)
        load_wt(0, 0)
        load_wt(0, 1)
        nc.sync.dma_start(pos1_sb[:], pos1)
        nc.sync.dma_start(pos2_sb[:], pos2)
        load_scales(was, wat_scales.rearrange("e s (q r) c -> r q (e s) c", r=4))
        load_wa(0)
        load_wt(1, 0)
        load_wa(1)
        load_wt(1, 1)

        gbank = bank(7, "gbank")
        nc.tensor.transpose(gbank[:, 0:P], gate_rows, ident[:])
        nc.scalar.activation(out=gcol[:], in_=gbank[:, 0:E], func=COPY)

        gw = {}
        gs = {}
        for e0, e1 in GROUPS:
            n = C * (e1 - e0)
            cut = offs_sb[:, 8 * e0:8 * e1]
            for s in range(PASSES):
                if e0 == 0:
                    gw[e0, s] = sb([P, n], U32, "gw%d%d" % (e0, s))
                    gs[e0, s] = sb([P, n], U8, "gs%d%d" % (e0, s))
                else:
                    at = GATHERED_AT + 768 * (PASSES * (e0 - 2) + (e1 - e0) * s)
                    gw[e0, s] = place([P, n], U32, "gw%d%d" % (e0, s), at)
                    gs[e0, s] = place([P, n], U8, "gs%d%d" % (e0, s), at + 4 * n)
                nc.vector.tensor_copy(out=gw[e0, s][:], in_=dyw[s].bitcast(U32).indirect(cut))
                nc.vector.tensor_copy(out=gs[e0, s][:], in_=dys[:, s, :].indirect(cut))

        hc = {}
        dhts = {}
        hs = {}
        def weave_dh(g):
            e0, e1 = GROUPS[g]
            n = C * (e1 - e0)
            wbank = bank(TURN_BANKS[g], "wbank%d" % e0)
            for e in range(e0, e1):
                pairs = dhts[e][:].bitcast(F32)
                for u in range(2):
                    at = P * (2 * (e - e0) + u)
                    nc.tensor.transpose(wbank[:, at:at + P], pairs[:, P * u:P * (u + 1)], ident[:])
            dhb = sb([P, 4 * n], BF16, "dhb%d" % e0)
            weaver = nc.vector.tensor_copy if g == 2 else nc.scalar.copy
            weaver(
                out=dhb[:].bitcast(F32).rearrange("p (x c u) -> p x c u", c=C, u=2),
                in_=wbank[:, 0:2 * n].rearrange("p (x u c) -> p x c u", c=C, u=2))
            codes = sb([P, n], U32, "hc%d" % e0)
            scales = sb([P, n], U8, "hs%d" % e0)
            nc.vector.quantize_mx(out=codes[:].bitcast(FP8X4), scales=scales[:], in_=dhb[:])
            for e in range(e0, e1):
                hc[e] = codes[:, C * (e - e0):C * (e - e0 + 1)]
                hs[e] = scales[:, C * (e - e0):C * (e - e0 + 1)]

        for e0, e1 in GROUPS:
            for e in range(e0, e1):
                hbank = bank(SUM_BANKS[e], "hbank%d" % e)
                slots = slice(C * (e - e0), C * (e - e0 + 1))
                for s in range(PASSES):
                    at = 1024 * (2 * (e % 2) + s)
                    nc.tensor.matmul_mx(
                        out=hbank[:], lhsT=gw[e0, s][:, slots].bitcast(FP8X4), lhsT_scale=gs[e0, s][:, slots],
                        rhs=wb_words[e // 2][:, at:at + 1024].bitcast(FP4X4),
                        rhs_scale=wbs[e // 4][:, 2 * (e % 4) + s, :],
                        start=(s == 0), stop=(s == PASSES - 1))
                dht = sb([P, H], BF16, "dht%d" % e)
                nc.scalar.activation(
                    out=dht[:].rearrange("c (u p h) -> c u p h", u=2, h=2),
                    in_=hbank[:].rearrange("c (p u h) -> c u p h", u=2, h=2),
                    func=COPY, scale=gcol[:, e:e + 1])
                dhts[e] = dht
            for late in WOVEN_BEHIND.get(e1, ()):
                weave_dh(late)

        dx = [sb([P, S], F32, "dx%d" % b) for b in range(BLOCKS)]

        def adapters(b, e0, e1, number, copy):
            dbank = bank(number, "dbank%d%d" % (b, e0))
            for e in range(e0, e1):
                at = 512 * e + 2 * P * (b % 2)
                nc.tensor.matmul_mx(
                    out=dbank[:, C * (e - e0):C * (e - e0 + 1)],
                    lhsT=wa_words[b // 2][:, at:at + 2 * P].bitcast(FP4X4),
                    lhsT_scale=was[:, e, P * b:P * (b + 1)],
                    rhs=hc[e].bitcast(FP8X4), rhs_scale=hs[e], start=True, stop=True)
            copy(out=dx[b][:, C * e0:C * e1], in_=dbank[:, 0:C * (e1 - e0)])

        wc = {}
        ws = {}

        def round_wt(h, s, copy, at):
            wt16 = place([P, 1024], BF16, "wt16%d%d" % (h, s), at)
            copy(out=wt16[:].rearrange("p (c i j) -> p c j i", i=4, j=4),
                 in_=wraw[h, s][:].rearrange("p j (c i) -> p c j i", i=4))
            wc[h, s] = sb([P, 256], U32, "wc%d%d" % (h, s))
            ws[h, s] = sb([P, 256], U8, "ws%d%d" % (h, s))
            nc.vector.quantize_mx(out=wc[h, s][:].bitcast(FP8X4), scales=ws[h, s][:], in_=wt16[:])

        base = {}

        def frozen(b, number):
            base[b] = bank(number, "base%d" % b)
            cols = slice(P * (b % 2), P * (b % 2 + 1))
            for s in range(PASSES):
                nc.tensor.matmul_mx(
                    out=base[b][:], lhsT=wc[b // 2, s][:, cols].bitcast(FP8X4), lhsT_scale=ws[b // 2, s][:, cols],
                    rhs=dyw[s].bitcast(FP8X4), rhs_scale=dys[:, s, :], start=(s == 0), stop=(s == PASSES - 1))

        ys = sb([P, BLOCKS, P], U8, "ys")
        yt = [sb([P, K], BF16, "yt%d" % b) for b in range(BLOCKS)]
        yb = [sb([P, 4 * P], BF16, "yb%d" % b) for b in range(BLOCKS)]
        y = [sb([P, T], F32, "y%d" % b) for b in range(BLOCKS)]
        second = {}
        both = {}

        def gather_second(b):
            for h in range(2):
                at = SECOND_AT + 2048 * (2 * b + h)
                second[b, h] = place([P, 256], F32, "second%d%d" % (b, h), at)
                nc.scalar.activation(out=second[b, h][:], in_=dx[b][:].indirect(pos2_sb[:, 16 * h:16 * (h + 1)]),
                                     func=COPY)

        def gather_first(b, h):
            both[b, h] = place([P, 256], F32, "both%d%d" % (b, h), BOTH_AT + 1024 * ((2 * b + h) % 3))
            nc.vector.tensor_tensor(both[b, h][:], dx[b][:].indirect(pos1_sb[:, 16 * h:16 * (h + 1)]),
                                    second[b, h][:], ADD)

        def add_base(b, x0, x1):
            cols = slice(P * x0, P * x1)
            nc.vector.tensor_tensor(y[b][:, cols], both[b, x0 // 2][:, P * (x0 % 2):P * (x0 % 2 + x1 - x0)],
                                    base[b][:, cols], ADD)

        def turn(b, x0, x1, number, copy):
            if x1 == 4:
                nc.sync.dma_start(out=out_0[P * b:P * (b + 1), :], in_=y[b][:])
            tbank = bank(number, "tbank%d%d" % (b, x0))
            for x in range(x0, x1):
                nc.tensor.transpose(tbank[:, P * (x - x0):P * (x - x0 + 1)], y[b][:, P * x:P * (x + 1)], ident[:])
            copy(
                out=yt[b][:].rearrange("c (u p h) -> c u p h", u=2, h=2)[:, :, 32 * x0:32 * x1, :],
                in_=tbank[:, 0:P * (x1 - x0)].rearrange("c (p u h) -> c u p h", u=2, h=2))

        def planes(b, number, copy):
            xbank = bank(number, "xbank%d" % b)
            pairs = yt[b][:].bitcast(F32)
            for u in range(2):
                nc.tensor.transpose(xbank[:, P * u:P * (u + 1)], pairs[:, P * u:P * (u + 1)], ident[:])
            copy(out=yb[b][:].bitcast(F32).rearrange("p (c u) -> p c u", u=2),
                 in_=xbank[:, 0:2 * P].rearrange("p (u c) -> p c u", u=2))

        on_vector = nc.vector.tensor_copy
        on_scalar = nc.scalar.copy

        round_wt(0, 0, on_vector, WT16_AT)
        round_wt(0, 1, on_vector, WT16_AT + 2048)
        adapters(0, 0, 4, 5, on_scalar)
        adapters(0, 4, 7, 7, on_scalar)
        adapters(0, 7, 8, 2, on_scalar)
        round_wt(1, 0, on_vector, WT16_AT + 4096)
        gather_second(0)
        adapters(1, 0, 4, 2, on_scalar)
        adapters(1, 4, 8, 0, on_scalar)
        frozen(0, 5)
        gather_first(0, 0)
        gather_first(0, 1)
        frozen(1, 7)
        gather_second(1)
        adapters(2, 0, 4, 2, on_vector)
        adapters(2, 4, 8, 1, on_scalar)
        add_base(0, 0, 2)
        gather_first(1, 0)
        add_base(0, 2, 4)
        turn(0, 0, 4, 3, on_scalar)
        gather_first(1, 1)
        round_wt(1, 1, on_vector, SECOND_AT + 2 * 2048)
        gather_second(2)
        add_base(1, 0, 2)
        add_base(1, 2, 4)
        frozen(2, 6)
        frozen(3, 0)
        adapters(3, 0, 4, 2, on_scalar)
        adapters(3, 4, 8, 1, on_scalar)
        gather_second(3)
        turn(1, 0, 4, 4, on_scalar)
        gather_first(2, 0)
        gather_first(2, 1)
        planes(0, 5, on_scalar)
        add_base(2, 0, 2)
        gather_first(3, 0)
        add_base(2, 2, 4)
        turn(2, 0, 4, 3, on_scalar)
        gather_first(3, 1)
        planes(1, 7, on_scalar)
        add_base(3, 0, 2)
        add_base(3, 2, 4)
        turn(3, 0, 2, 4, on_scalar)
        turn(3, 2, 4, 1, on_vector)
        planes(2, 2, on_scalar)
        planes(3, 5, on_vector)

        yc = place([P, BLOCKS, P], U32, "yc", SECOND_AT + 2048 * 7)
        for b in range(BLOCKS):
            nc.vector.quantize_mx(out=yc[:, b, :].bitcast(FP8X4), scales=ys[:, b, :], in_=yb[b][:])
        word_rows = out_1[0].rearrange("p t d -> p (t d)").bitcast(I32).rearrange("(b q) t -> q b t", b=BLOCKS)
        scale_rows = out_2[0].rearrange("(b g) t -> g b t", g=4)
        for x in (0, 2, 1, 3):
            nc.sync.dma_start(out=word_rows[:, :, P * x:P * (x + 1)], in_=yc[32 * x:32 * (x + 1)].bitcast(I32))
            nc.scalar.dma_start(out=scale_rows[:, :, P * x:P * (x + 1)].bitcast(I32),
                                in_=ys[32 * x:32 * x + 4].bitcast(I32))
